import numpy as np
import ml_dtypes


def mxq(x, axis, fmt="e4m3"):
    dtype, down = {"e4m3": (ml_dtypes.float8_e4m3fn, 7), "e5m2": (ml_dtypes.float8_e5m2, 14)}[fmt]
    v = np.moveaxis(np.asarray(x, np.float32).astype(ml_dtypes.bfloat16).astype(np.float64), axis, -1)
    blocks = v.reshape(v.shape[:-1] + (-1, 32))
    amax = np.abs(blocks).max(-1, keepdims=True)
    byte = np.maximum(np.where(amax > 0, np.frexp(amax)[1] - 1 + 127, 0) - down, 1)
    scale = np.exp2(byte - 127.0)
    codes = (blocks / scale).astype(np.float32).astype(dtype).astype(np.float64)
    return np.moveaxis((codes * scale).reshape(v.shape), -1, axis)


WIDE = False


def mx_kscale(k, group=512):
    if not WIDE:
        return np.ones(k)
    levels = np.array([18, -18])
    if group != 512:
        return np.exp2(np.random.permutation(np.resize(levels, k // group))).repeat(group)
    if k % 512:
        return np.exp2(np.random.permutation(np.resize(levels, k // 32))).repeat(32)
    a = np.empty((k // 512, 16))
    for p in range(k // 512):
        a[p, :8] = np.random.permutation(np.resize(levels, 8))
        for g in range(8):
            far = levels[np.abs(levels - a[p, g]) >= 10]
            a[p, g + 8] = far[np.random.randint(len(far))]
    return np.exp2(a.ravel()).repeat(32)


def f64(x):
    return np.asarray(x).astype(np.float64)


E2M1 = np.array([0.0, 0.5, 1.0, 1.5, 2.0, 3.0, 4.0, 6.0, -0.0, -0.5, -1.0, -1.5, -2.0, -3.0, -4.0, -6.0])


def pack_group(w):
    k, n = w.shape
    w = f64(np.asarray(w, np.float32).astype(ml_dtypes.bfloat16)).reshape(k // 32, 32, n)
    amax = np.abs(w).max(1)
    mant, ex = np.frexp(amax / 6.0)
    byte = np.clip(np.where(amax > 0, np.where(mant > 0.5, ex, ex - 1) + 127, 1), 1, 254)
    scaled = (w * np.exp2(127.0 - byte)[:, None, :]).reshape(k, n).astype(np.float32)
    c = np.ascontiguousarray(scaled.reshape(k // 4, 4, n).transpose(0, 2, 1)).astype(ml_dtypes.float4_e2m1fn).view(np.uint8) & 0xF
    return np.ascontiguousarray((c[..., 0::2] | (c[..., 1::2] << 4)).reshape(k // 4, 2 * n)), byte.astype(np.uint8)


def unpack_group(words, scales):
    p, n = words.shape[0], scales.shape[1]
    words = np.ascontiguousarray(words).reshape(p, n, 2)
    nib = np.empty((p, n, 4), np.uint8)
    nib[..., 0::2] = words & 0xF
    nib[..., 1::2] = words >> 4
    return E2M1[nib].transpose(0, 2, 1).reshape(4 * p, n) * np.repeat(np.exp2(scales.astype(np.float64) - 127.0), 32, axis=0)


def silu(v):
    return v / (1.0 + np.exp(-v))


G, D, M, N = 4, 128, 256, 512


def setup_inputs():
    n = np.random.standard_normal
    s = mx_kscale(D, 0)[:, None]
    w_ = [pack_group(w) for w in n((G, D, M)) / np.sqrt(D) / s]
    u_ = [pack_group(w) for w in n((G, D, M)) / np.sqrt(D) / s]
    return {
        "x": (n((G, D, N)) * s).astype(np.float32),
        "w_words": np.stack([w[0] for w in w_]),
        "w_scales": np.stack([w[1] for w in w_]),
        "u_words": np.stack([w[0] for w in u_]),
        "u_scales": np.stack([w[1] for w in u_]),
    }


def reference(x, w_words, w_scales, u_words, u_scales):
    xq = mxq(f64(x), 1, "e4m3")
    h = np.stack([unpack_group(w_words[g], w_scales[g]) for g in range(G)]).transpose(0, 2, 1) @ xq
    g = np.stack([unpack_group(u_words[g], u_scales[g]) for g in range(G)]).transpose(0, 2, 1) @ xq
    y = silu(h) * g
    return y

@@ -1,0 +1,152 @@
+from contextlib import ExitStack
+
+import concourse.mybir as mybir
+
+G, D, M, N = 4, 128, 256, 512
+FLOPS = 2 * 2 * G * D * M * N
+
+F32 = mybir.dt.float32
+BF16 = mybir.dt.bfloat16
+I32 = mybir.dt.int32
+U32 = mybir.dt.uint32
+U8 = mybir.dt.uint8
+FP8X4 = mybir.dt.float8_e4m3fn_x4
+FP4X4 = mybir.dt.float4_e2m1fn_x4
+SILU = mybir.ActivationFunctionType.Silu
+MULT = mybir.AluOpType.mult
+
+P = 128
+PACK = 4
+ROWS = D // PACK
+SCALE_ROWS = D // 32
+HALF = N // 2
+M_TILE = 128
+VECTOR_COLS = 176
+
+
+def tile_rows_gglu_silu_kernel(tc, x, w_words, w_scales, u_words, u_scales, out):
+    nc = tc.nc
+    with ExitStack() as ctx:
+        keep = ctx.enter_context(tc.tile_pool(name="keep", bufs=1))
+        psum = ctx.enter_context(tc.psum_pool(name="psum", bufs=1))
+        ctx.enter_context(tc.manual_schedule())
+
+        raw = [keep.tile([P, PACK, HALF], F32, name=f"raw{h}", align_bytes=64) for h in range(2)]
+        grouped = [keep.tile([P, HALF, PACK], BF16, name=f"grouped{h}", align_bytes=64) for h in range(2)]
+        x_codes = keep.tile([P, 3 * HALF], U32, align_bytes=64)
+        x_scales = keep.tile([P, 3 * HALF], U8, align_bytes=64)
+        words = [keep.tile([P, 2 * M], U8, name=f"words{i}", align_bytes=64) for i in range(2)]
+        planes = keep.tile([P, 2, M], U8, align_bytes=64)
+        warm_in = keep.tile([P, 8], F32)
+        warm_out = keep.tile([P, 8], F32)
+        banks = [[psum.tile([M_TILE, N], F32, name=f"bank{i}{g}") for g in range(G)] for i in range(2)]
+
+        x_rows = x.rearrange("g (p j) n -> (g p) j n", j=PACK)
+
+        def load_x(h):
+            nc.sync.dma_start(out=raw[h][:], in_=x_rows[:, :, h * HALF : (h + 1) * HALF])
+
+        def load_words(i, src):
+            nc.sync.dma_start(out=words[i][:].bitcast(I32), in_=src.rearrange("g p b -> (g p) b").bitcast(I32))
+
+        def load_scales(queue, g):
+            for i, src in enumerate((w_scales, u_scales)):
+                queue.dma_start(
+                    out=planes[ROWS * g : ROWS * g + SCALE_ROWS, i, :].bitcast(I32), in_=src[g].bitcast(I32)
+                )
+
+        def interleave(h, c0, c1, on_vector):
+            dst = grouped[h][:, c0:c1, :].rearrange("p (c i) j -> p c j i", i=4)
+            src = raw[h][:, :, c0:c1].rearrange("p j (c i) -> p c j i", i=4)
+            if on_vector:
+                nc.vector.tensor_copy(out=dst, in_=src)
+            else:
+                nc.scalar.copy(out=dst, in_=src)
+
+        def quantize(h):
+            cols = slice(2 * h * HALF, (2 * h + 1) * HALF)
+            nc.vector.quantize_mx(
+                out=x_codes[:, cols].bitcast(FP8X4),
+                scales=x_scales[:, cols],
+                in_=grouped[h][:].rearrange("p n j -> p (n j)"),
+            )
+
+        units = [(h, m, g) for h in range(2) for m in range(2) for g in range(G)]
+
+        def multiply(i, unit):
+            h, m, g = unit
+            rows = slice(ROWS * g, ROWS * (g + 1))
+            window = slice(h * HALF, h * HALF + N)
+            nc.tensor.matmul_mx(
+                out=banks[i][g][:],
+                lhsT=words[i][rows, 2 * M_TILE * m : 2 * M_TILE * (m + 1)].bitcast(FP4X4),
+                lhsT_scale=planes[rows, i, M_TILE * m : M_TILE * (m + 1)],
+                rhs=x_codes[rows, window].bitcast(FP8X4),
+                rhs_scale=x_scales[rows, window],
+                start=True,
+                stop=True,
+            )
+
+        load_x(0)
+        nc.vector.memset(planes[:].rearrange("p i m -> p (i m)").bitcast(I32), 0)
+        nc.vector.memset(warm_in[:], 0.0)
+        nc.vector.memset(x_codes[:, HALF : 2 * HALF], 0)
+        nc.vector.memset(x_scales[:, HALF : 2 * HALF].bitcast(I32), 0)
+        load_words(0, w_words)
+        load_words(1, u_words)
+        load_x(1)
+        load_scales(nc.scalar, 0)
+        load_scales(nc.scalar, 1)
+        load_scales(nc.gpsimd, 2)
+        nc.scalar.activation(out=warm_out[:], in_=warm_in[:], func=SILU)
+        load_scales(nc.scalar, 3)
+
+        interleave(0, 0, VECTOR_COLS, True)
+        interleave(0, VECTOR_COLS, HALF, False)
+        quantize(0)
+        interleave(1, 0, HALF, True)
+
+        for i in range(2):
+            for unit in units[:G]:
+                multiply(i, unit)
+
+        gates = [keep.tile([P, HALF], F32, name=f"gate{k}") for k in range(len(units))]
+        results = [keep.tile([P, 2, HALF], F32, name=f"result{k}") for k in range(len(units) // 2)]
+
+        def activate(k):
+            h, m, g = units[k]
+            nc.scalar.activation(out=gates[k][:], in_=banks[0][g][:, h * HALF : (h + 1) * HALF], func=SILU)
+
+        def store(k0, k1):
+            h, m, g = units[k0]
+            nc.sync.dma_start(
+                out=out[g : g + k1 - k0, M_TILE * m : M_TILE * (m + 1), h * HALF : (h + 1) * HALF].rearrange(
+                    "g p n -> p g n"
+                ),
+                in_=results[k0 // 2][:, k0 % 2 : k0 % 2 + k1 - k0, :],
+            )
+
+        def combine(k):
+            h, m, g = units[k]
+            nc.vector.tensor_tensor(
+                out=results[k // 2][:, k % 2, :],
+                in0=banks[1][g][:, h * HALF : (h + 1) * HALF],
+                in1=gates[k][:],
+                op=MULT,
+            )
+            if k >= len(units) - 2:
+                store(k, k + 1)
+            elif k % 2 == 1:
+                store(k - 1, k + 1)
+
+        for k in range(len(units) + 1):
+            if k < len(units):
+                activate(k)
+                if k + G < len(units):
+                    multiply(0, units[k + G])
+            if k >= 1:
+                combine(k - 1)
+                if k == 2:
+                    quantize(1)
+                if k - 1 + G < len(units):
+                    multiply(1, units[k - 1 + G])

@@ -21,7 +21,7 @@ ROWS = D // PACK
 SCALE_ROWS = D // 32
 HALF = N // 2
 M_TILE = 128
-VECTOR_COLS = 176
+QUARTER = N // 4
 
 
 def tile_rows_gglu_silu_kernel(tc, x, w_words, w_scales, u_words, u_scales, out):
@@ -49,34 +49,38 @@ def tile_rows_gglu_silu_kernel(tc, x, w_words, w_scales, u_words, u_scales, out)
         def load_words(i, src):
             nc.sync.dma_start(out=words[i][:].bitcast(I32), in_=src.rearrange("g p b -> (g p) b").bitcast(I32))
 
-        def load_scales(queue, g):
-            for i, src in enumerate((w_scales, u_scales)):
-                queue.dma_start(
-                    out=planes[ROWS * g : ROWS * g + SCALE_ROWS, i, :].bitcast(I32), in_=src[g].bitcast(I32)
-                )
+        def load_scales(queue, g, i):
+            src = (w_scales, u_scales)[i]
+            queue.dma_start(out=planes[ROWS * g : ROWS * g + SCALE_ROWS, i, :].bitcast(I32), in_=src[g].bitcast(I32))
 
-        def interleave(h, c0, c1, on_vector):
-            dst = grouped[h][:, c0:c1, :].rearrange("p (c i) j -> p c j i", i=4)
-            src = raw[h][:, :, c0:c1].rearrange("p j (c i) -> p c j i", i=4)
-            if on_vector:
-                nc.vector.tensor_copy(out=dst, in_=src)
-            else:
-                nc.scalar.copy(out=dst, in_=src)
-
-        def quantize(h):
-            cols = slice(2 * h * HALF, (2 * h + 1) * HALF)
-            nc.vector.quantize_mx(
-                out=x_codes[:, cols].bitcast(FP8X4),
-                scales=x_scales[:, cols],
-                in_=grouped[h][:].rearrange("p n j -> p (n j)"),
+        def interleave(copy, h, q):
+            cols = slice(q * QUARTER, (q + 1) * QUARTER)
+            copy(
+                out=grouped[h][:, cols, :].rearrange("p (c i) j -> p c j i", i=4),
+                in_=raw[h][:, :, cols].rearrange("p j (c i) -> p c j i", i=4),
             )
 
-        units = [(h, m, g) for h in range(2) for m in range(2) for g in range(G)]
+        def quantize(h, q):
+            first = (h + 1) * HALF + q * QUARTER
+            nc.vector.quantize_mx(
+                out=x_codes[:, first : first + QUARTER].bitcast(FP8X4),
+                scales=x_scales[:, first : first + QUARTER],
+                in_=grouped[h][:, q * QUARTER : (q + 1) * QUARTER, :].rearrange("p n j -> p (n j)"),
+            )
 
-        def multiply(i, unit):
-            h, m, g = unit
+        units = (
+            [(g, 0, 0, HALF) for g in range(G)]
+            + [(g, 1, 0, HALF) for g in range(2)]
+            + [(g, 1, 0, N) for g in range(2, G)]
+            + [(g, 0, HALF, N) for g in range(G)]
+            + [(g, 1, HALF, N) for g in range(2)]
+        )
+        stores = [(0, 2), (2, 4), (4, 6), (6, 7), (7, 8), (8, 10), (10, 12), (12, 13), (13, 14)]
+
+        def multiply(i, k):
+            g, m, c0, c1 = units[k]
             rows = slice(ROWS * g, ROWS * (g + 1))
-            window = slice(h * HALF, h * HALF + N)
+            window = slice(0, N) if c1 == HALF else slice(HALF, HALF + N)
             nc.tensor.matmul_mx(
                 out=banks[i][g][:],
                 lhsT=words[i][rows, 2 * M_TILE * m : 2 * M_TILE * (m + 1)].bitcast(FP4X4),
@@ -87,66 +91,60 @@ def tile_rows_gglu_silu_kernel(tc, x, w_words, w_scales, u_words, u_scales, out)
                 stop=True,
             )
 
+        def sums(i, k):
+            g, m, c0, c1 = units[k]
+            return banks[i][g][:, N - (c1 - c0) : N]
+
         load_x(0)
         nc.vector.memset(planes[:].rearrange("p i m -> p (i m)").bitcast(I32), 0)
         nc.vector.memset(warm_in[:], 0.0)
-        nc.vector.memset(x_codes[:, HALF : 2 * HALF], 0)
-        nc.vector.memset(x_scales[:, HALF : 2 * HALF].bitcast(I32), 0)
+        nc.vector.memset(x_codes[:, 0:HALF], 0)
+        nc.vector.memset(x_scales[:, 0:HALF].bitcast(I32), 0)
         load_words(0, w_words)
         load_words(1, u_words)
         load_x(1)
-        load_scales(nc.scalar, 0)
-        load_scales(nc.scalar, 1)
-        load_scales(nc.gpsimd, 2)
+        for g in range(G):
+            load_scales(nc.scalar, g, 0)
+        for g in range(G):
+            load_scales(nc.gpsimd if g < 2 else nc.sync, g, 1)
         nc.scalar.activation(out=warm_out[:], in_=warm_in[:], func=SILU)
-        load_scales(nc.scalar, 3)
 
-        interleave(0, 0, VECTOR_COLS, True)
-        interleave(0, VECTOR_COLS, HALF, False)
-        quantize(0)
-        interleave(1, 0, HALF, True)
+        interleave(nc.vector.tensor_copy, 0, 0)
+        interleave(nc.scalar.copy, 0, 1)
+        quantize(0, 0)
+        quantize(0, 1)
+        interleave(nc.vector.tensor_copy, 1, 0)
+        interleave(nc.vector.tensor_copy, 1, 1)
+        quantize(1, 0)
+        quantize(1, 1)
 
         for i in range(2):
-            for unit in units[:G]:
-                multiply(i, unit)
+            for k in range(G):
+                multiply(i, k)
 
-        gates = [keep.tile([P, HALF], F32, name=f"gate{k}") for k in range(len(units))]
-        results = [keep.tile([P, 2, HALF], F32, name=f"result{k}") for k in range(len(units) // 2)]
-
-        def activate(k):
-            h, m, g = units[k]
-            nc.scalar.activation(out=gates[k][:], in_=banks[0][g][:, h * HALF : (h + 1) * HALF], func=SILU)
-
-        def store(k0, k1):
-            h, m, g = units[k0]
-            nc.sync.dma_start(
-                out=out[g : g + k1 - k0, M_TILE * m : M_TILE * (m + 1), h * HALF : (h + 1) * HALF].rearrange(
-                    "g p n -> p g n"
-                ),
-                in_=results[k0 // 2][:, k0 % 2 : k0 % 2 + k1 - k0, :],
-            )
+        gates = [keep.tile([P, c1 - c0], F32, name=f"gate{k}") for k, (g, m, c0, c1) in enumerate(units)]
+        results = {}
+        for k0, k1 in stores:
+            staged = keep.tile([P, k1 - k0, units[k0][3] - units[k0][2]], F32, name=f"result{k0}")
+            for k in range(k0, k1):
+                results[k] = (staged, k0, k1)
 
         def combine(k):
-            h, m, g = units[k]
-            nc.vector.tensor_tensor(
-                out=results[k // 2][:, k % 2, :],
-                in0=banks[1][g][:, h * HALF : (h + 1) * HALF],
-                in1=gates[k][:],
-                op=MULT,
-            )
-            if k >= len(units) - 2:
-                store(k, k + 1)
-            elif k % 2 == 1:
-                store(k - 1, k + 1)
+            staged, k0, k1 = results[k]
+            nc.vector.tensor_tensor(out=staged[:, k - k0, :], in0=sums(1, k), in1=gates[k][:], op=MULT)
+            if k == k1 - 1:
+                g, m, c0, c1 = units[k0]
+                nc.sync.dma_start(
+                    out=out[g : g + k1 - k0, M_TILE * m : M_TILE * (m + 1), c0:c1].rearrange("g p n -> p g n"),
+                    in_=staged[:],
+                )
 
         for k in range(len(units) + 1):
             if k < len(units):
-                activate(k)
+                nc.scalar.activation(out=gates[k][:], in_=sums(0, k), func=SILU)
                 if k + G < len(units):
-                    multiply(0, units[k + G])
+                    multiply(0, k + G)
             if k >= 1:
                 combine(k - 1)
-                if k == 2:
-                    quantize(1)
                 if k - 1 + G < len(units):
-                    multiply(1, units[k - 1 + G])
+                    multiply(1, k - 1 + G)

@@ -101,10 +101,10 @@ def tile_rows_gglu_silu_kernel(tc, x, w_words, w_scales, u_words, u_scales, out)
         nc.vector.memset(x_codes[:, 0:HALF], 0)
         nc.vector.memset(x_scales[:, 0:HALF].bitcast(I32), 0)
         load_words(0, w_words)
+        for g in range(G):
+            load_scales(nc.sync, g, 0)
         load_words(1, u_words)
         load_x(1)
-        for g in range(G):
-            load_scales(nc.scalar, g, 0)
         for g in range(G):
             load_scales(nc.gpsimd if g < 2 else nc.sync, g, 1)
         nc.scalar.activation(out=warm_out[:], in_=warm_in[:], func=SILU)

@@ -22,6 +22,7 @@ SCALE_ROWS = D // 32
 HALF = N // 2
 M_TILE = 128
 QUARTER = N // 4
+SCALAR_COLS = 64
 
 
 def tile_rows_gglu_silu_kernel(tc, x, w_words, w_scales, u_words, u_scales, out):
@@ -53,8 +54,8 @@ def tile_rows_gglu_silu_kernel(tc, x, w_words, w_scales, u_words, u_scales, out)
             src = (w_scales, u_scales)[i]
             queue.dma_start(out=planes[ROWS * g : ROWS * g + SCALE_ROWS, i, :].bitcast(I32), in_=src[g].bitcast(I32))
 
-        def interleave(copy, h, q):
-            cols = slice(q * QUARTER, (q + 1) * QUARTER)
+        def interleave(copy, h, c0, c1):
+            cols = slice(c0, c1)
             copy(
                 out=grouped[h][:, cols, :].rearrange("p (c i) j -> p c j i", i=4),
                 in_=raw[h][:, :, cols].rearrange("p j (c i) -> p c j i", i=4),
@@ -68,19 +69,17 @@ def tile_rows_gglu_silu_kernel(tc, x, w_words, w_scales, u_words, u_scales, out)
                 in_=grouped[h][:, q * QUARTER : (q + 1) * QUARTER, :].rearrange("p n j -> p (n j)"),
             )
 
-        units = (
-            [(g, 0, 0, HALF) for g in range(G)]
-            + [(g, 1, 0, HALF) for g in range(2)]
-            + [(g, 1, 0, N) for g in range(2, G)]
-            + [(g, 0, HALF, N) for g in range(G)]
-            + [(g, 1, HALF, N) for g in range(2)]
+        passes = (
+            [(g, 0, (0,)) for g in range(G)]
+            + [(g, 1, (0, 1)) for g in range(G)]
+            + [(g, 0, (1,)) for g in range(G)]
         )
-        stores = [(0, 2), (2, 4), (4, 6), (6, 7), (7, 8), (8, 10), (10, 12), (12, 13), (13, 14)]
+        steps = [(k, h) for k, (g, m, halves) in enumerate(passes) for h in halves]
 
         def multiply(i, k):
-            g, m, c0, c1 = units[k]
+            g, m, halves = passes[k]
             rows = slice(ROWS * g, ROWS * (g + 1))
-            window = slice(0, N) if c1 == HALF else slice(HALF, HALF + N)
+            window = slice(0, N) if halves == (0,) else slice(HALF, HALF + N)
             nc.tensor.matmul_mx(
                 out=banks[i][g][:],
                 lhsT=words[i][rows, 2 * M_TILE * m : 2 * M_TILE * (m + 1)].bitcast(FP4X4),
@@ -91,9 +90,10 @@ def tile_rows_gglu_silu_kernel(tc, x, w_words, w_scales, u_words, u_scales, out)
                 stop=True,
             )
 
-        def sums(i, k):
-            g, m, c0, c1 = units[k]
-            return banks[i][g][:, N - (c1 - c0) : N]
+        def sums(i, k, h):
+            g, m, halves = passes[k]
+            first = HALF if halves == (0,) else h * HALF
+            return banks[i][g][:, first : first + HALF]
 
         load_x(0)
         nc.vector.memset(planes[:].rearrange("p i m -> p (i m)").bitcast(I32), 0)
@@ -109,12 +109,13 @@ def tile_rows_gglu_silu_kernel(tc, x, w_words, w_scales, u_words, u_scales, out)
             load_scales(nc.gpsimd if g < 2 else nc.sync, g, 1)
         nc.scalar.activation(out=warm_out[:], in_=warm_in[:], func=SILU)
 
-        interleave(nc.vector.tensor_copy, 0, 0)
-        interleave(nc.scalar.copy, 0, 1)
+        interleave(nc.vector.tensor_copy, 0, 0, QUARTER)
+        interleave(nc.scalar.copy, 0, QUARTER, HALF)
         quantize(0, 0)
         quantize(0, 1)
-        interleave(nc.vector.tensor_copy, 1, 0)
-        interleave(nc.vector.tensor_copy, 1, 1)
+        interleave(nc.vector.tensor_copy, 1, 0, QUARTER)
+        interleave(nc.vector.tensor_copy, 1, QUARTER, HALF - SCALAR_COLS)
+        interleave(nc.scalar.copy, 1, HALF - SCALAR_COLS, HALF)
         quantize(1, 0)
         quantize(1, 1)
 
@@ -122,29 +123,29 @@ def tile_rows_gglu_silu_kernel(tc, x, w_words, w_scales, u_words, u_scales, out)
             for k in range(G):
                 multiply(i, k)
 
-        gates = [keep.tile([P, c1 - c0], F32, name=f"gate{k}") for k, (g, m, c0, c1) in enumerate(units)]
-        results = {}
-        for k0, k1 in stores:
-            staged = keep.tile([P, k1 - k0, units[k0][3] - units[k0][2]], F32, name=f"result{k0}")
-            for k in range(k0, k1):
-                results[k] = (staged, k0, k1)
+        gates = [keep.tile([P, HALF], F32, name=f"gate{s}") for s in range(len(steps))]
+        results = [keep.tile([P, HALF * len(halves)], F32, name=f"result{k}") for k, (g, m, halves) in enumerate(passes)]
 
-        def combine(k):
-            staged, k0, k1 = results[k]
-            nc.vector.tensor_tensor(out=staged[:, k - k0, :], in0=sums(1, k), in1=gates[k][:], op=MULT)
-            if k == k1 - 1:
-                g, m, c0, c1 = units[k0]
+        def activate(s):
+            k, h = steps[s]
+            nc.scalar.activation(out=gates[s][:], in_=sums(0, k, h), func=SILU)
+            if h == passes[k][2][-1] and k + G < len(passes):
+                multiply(0, k + G)
+
+        def combine(s):
+            k, h = steps[s]
+            g, m, halves = passes[k]
+            place = (h - halves[0]) * HALF
+            nc.vector.tensor_tensor(out=results[k][:, place : place + HALF], in0=sums(1, k, h), in1=gates[s][:], op=MULT)
+            if h == halves[-1]:
                 nc.sync.dma_start(
-                    out=out[g : g + k1 - k0, M_TILE * m : M_TILE * (m + 1), c0:c1].rearrange("g p n -> p g n"),
-                    in_=staged[:],
+                    out=out[g, M_TILE * m : M_TILE * (m + 1), halves[0] * HALF : (h + 1) * HALF], in_=results[k][:]
                 )
+                if k + G < len(passes):
+                    multiply(1, k + G)
 
-        for k in range(len(units) + 1):
-            if k < len(units):
-                nc.scalar.activation(out=gates[k][:], in_=sums(0, k), func=SILU)
-                if k + G < len(units):
-                    multiply(0, k + G)
-            if k >= 1:
-                combine(k - 1)
-                if k - 1 + G < len(units):
-                    multiply(1, k - 1 + G)
+        for s in range(len(steps) + 1):
+            if s < len(steps):
+                activate(s)
+            if s >= 1:
+                combine(s - 1)

@@ -103,14 +103,15 @@ def tile_rows_gglu_silu_kernel(tc, x, w_words, w_scales, u_words, u_scales, out)
         load_words(0, w_words)
         for g in range(G):
             load_scales(nc.sync, g, 0)
-        load_words(1, u_words)
         load_x(1)
+        load_words(1, u_words)
         for g in range(G):
             load_scales(nc.gpsimd if g < 2 else nc.sync, g, 1)
         nc.scalar.activation(out=warm_out[:], in_=warm_in[:], func=SILU)
 
         interleave(nc.vector.tensor_copy, 0, 0, QUARTER)
-        interleave(nc.scalar.copy, 0, QUARTER, HALF)
+        interleave(nc.vector.tensor_copy, 0, QUARTER, HALF - SCALAR_COLS)
+        interleave(nc.scalar.copy, 0, HALF - SCALAR_COLS, HALF)
         quantize(0, 0)
         quantize(0, 1)
         interleave(nc.vector.tensor_copy, 1, 0, QUARTER)
@@ -137,12 +138,14 @@ def tile_rows_gglu_silu_kernel(tc, x, w_words, w_scales, u_words, u_scales, out)
             g, m, halves = passes[k]
             place = (h - halves[0]) * HALF
             nc.vector.tensor_tensor(out=results[k][:, place : place + HALF], in0=sums(1, k, h), in1=gates[s][:], op=MULT)
-            if h == halves[-1]:
+            if h == halves[-1] or k == G:
+                first = place if k == G else 0
                 nc.sync.dma_start(
-                    out=out[g, M_TILE * m : M_TILE * (m + 1), halves[0] * HALF : (h + 1) * HALF], in_=results[k][:]
+                    out=out[g, M_TILE * m : M_TILE * (m + 1), halves[0] * HALF + first : (h + 1) * HALF],
+                    in_=results[k][:, first : place + HALF],
                 )
-                if k + G < len(passes):
-                    multiply(1, k + G)
+            if h == halves[-1] and k + G < len(passes):
+                multiply(1, k + G)
 
         for s in range(len(steps) + 1):
             if s < len(steps):

@@ -50,9 +50,9 @@ def tile_rows_gglu_silu_kernel(tc, x, w_words, w_scales, u_words, u_scales, out)
         def load_words(i, src):
             nc.sync.dma_start(out=words[i][:].bitcast(I32), in_=src.rearrange("g p b -> (g p) b").bitcast(I32))
 
-        def load_scales(queue, g, i):
+        def load_scales(g, i):
             src = (w_scales, u_scales)[i]
-            queue.dma_start(out=planes[ROWS * g : ROWS * g + SCALE_ROWS, i, :].bitcast(I32), in_=src[g].bitcast(I32))
+            nc.sync.dma_start(out=planes[ROWS * g : ROWS * g + SCALE_ROWS, i, :].bitcast(I32), in_=src[g].bitcast(I32))
 
         def interleave(copy, h, c0, c1):
             cols = slice(c0, c1)
@@ -102,11 +102,12 @@ def tile_rows_gglu_silu_kernel(tc, x, w_words, w_scales, u_words, u_scales, out)
         nc.vector.memset(x_scales[:, 0:HALF].bitcast(I32), 0)
         load_words(0, w_words)
         for g in range(G):
-            load_scales(nc.sync, g, 0)
+            load_scales(g, 0)
+        load_scales(0, 1)
         load_x(1)
         load_words(1, u_words)
-        for g in range(G):
-            load_scales(nc.gpsimd if g < 2 else nc.sync, g, 1)
+        for g in range(1, G):
+            load_scales(g, 1)
         nc.scalar.activation(out=warm_out[:], in_=warm_in[:], func=SILU)
 
         interleave(nc.vector.tensor_copy, 0, 0, QUARTER)
@@ -138,14 +139,12 @@ def tile_rows_gglu_silu_kernel(tc, x, w_words, w_scales, u_words, u_scales, out)
             g, m, halves = passes[k]
             place = (h - halves[0]) * HALF
             nc.vector.tensor_tensor(out=results[k][:, place : place + HALF], in0=sums(1, k, h), in1=gates[s][:], op=MULT)
-            if h == halves[-1] or k == G:
-                first = place if k == G else 0
+            if h == halves[-1]:
                 nc.sync.dma_start(
-                    out=out[g, M_TILE * m : M_TILE * (m + 1), halves[0] * HALF + first : (h + 1) * HALF],
-                    in_=results[k][:, first : place + HALF],
+                    out=out[g, M_TILE * m : M_TILE * (m + 1), halves[0] * HALF : (h + 1) * HALF], in_=results[k][:]
                 )
-            if h == halves[-1] and k + G < len(passes):
-                multiply(1, k + G)
+                if k + G < len(passes):
+                    multiply(1, k + G)
 
         for s in range(len(steps) + 1):
             if s < len(steps):

@@ -19,10 +19,11 @@ P = 128
 PACK = 4
 ROWS = D // PACK
 SCALE_ROWS = D // 32
-HALF = N // 2
 M_TILE = 128
+HALF = N // 2
 QUARTER = N // 4
-SCALAR_COLS = 64
+RUN = 4
+W, U = 0, 1
 
 
 def tile_rows_gglu_silu_kernel(tc, x, w_words, w_scales, u_words, u_scales, out):
@@ -34,31 +35,32 @@ def tile_rows_gglu_silu_kernel(tc, x, w_words, w_scales, u_words, u_scales, out)
 
         raw = [keep.tile([P, PACK, HALF], F32, name=f"raw{h}", align_bytes=64) for h in range(2)]
         grouped = [keep.tile([P, HALF, PACK], BF16, name=f"grouped{h}", align_bytes=64) for h in range(2)]
-        x_codes = keep.tile([P, 3 * HALF], U32, align_bytes=64)
-        x_scales = keep.tile([P, 3 * HALF], U8, align_bytes=64)
-        words = [keep.tile([P, 2 * M], U8, name=f"words{i}", align_bytes=64) for i in range(2)]
-        planes = keep.tile([P, 2, M], U8, align_bytes=64)
-        warm_in = keep.tile([P, 8], F32)
-        warm_out = keep.tile([P, 8], F32)
-        banks = [[psum.tile([M_TILE, N], F32, name=f"bank{i}{g}") for g in range(G)] for i in range(2)]
+        x_codes = keep.tile([P, HALF + N], U32, align_bytes=64)
+        x_scales = keep.tile([P, HALF + N], U8, align_bytes=64)
+        words = [keep.tile([P, 2 * M], U8, name=f"words{i}", align_bytes=64) for i in (W, U)]
+        weight_scales = keep.tile([P, 2, M], U8, align_bytes=64)
+        banks = [[psum.tile([M_TILE, N], F32, name=f"bank{i}{g}") for g in range(G)] for i in (W, U)]
 
         x_rows = x.rearrange("g (p j) n -> (g p) j n", j=PACK)
 
         def load_x(h):
             nc.sync.dma_start(out=raw[h][:], in_=x_rows[:, :, h * HALF : (h + 1) * HALF])
 
-        def load_words(i, src):
+        def load_words(i):
+            src = (w_words, u_words)[i]
             nc.sync.dma_start(out=words[i][:].bitcast(I32), in_=src.rearrange("g p b -> (g p) b").bitcast(I32))
 
-        def load_scales(g, i):
+        def load_scales(i, g):
             src = (w_scales, u_scales)[i]
-            nc.sync.dma_start(out=planes[ROWS * g : ROWS * g + SCALE_ROWS, i, :].bitcast(I32), in_=src[g].bitcast(I32))
+            nc.sync.dma_start(
+                out=weight_scales[ROWS * g : ROWS * g + SCALE_ROWS, i, :].bitcast(I32), in_=src[g].bitcast(I32)
+            )
 
-        def interleave(copy, h, c0, c1):
-            cols = slice(c0, c1)
-            copy(
-                out=grouped[h][:, cols, :].rearrange("p (c i) j -> p c j i", i=4),
-                in_=raw[h][:, :, cols].rearrange("p j (c i) -> p c j i", i=4),
+        def interleave(h, q):
+            cols = slice(q * QUARTER, (q + 1) * QUARTER)
+            nc.vector.tensor_copy(
+                out=grouped[h][:, cols, :].rearrange("p (c i) j -> p c j i", i=RUN),
+                in_=raw[h][:, :, cols].rearrange("p j (c i) -> p c j i", i=RUN),
             )
 
         def quantize(h, q):
@@ -69,85 +71,70 @@ def tile_rows_gglu_silu_kernel(tc, x, w_words, w_scales, u_words, u_scales, out)
                 in_=grouped[h][:, q * QUARTER : (q + 1) * QUARTER, :].rearrange("p n j -> p (n j)"),
             )
 
-        passes = (
-            [(g, 0, (0,)) for g in range(G)]
-            + [(g, 1, (0, 1)) for g in range(G)]
-            + [(g, 0, (1,)) for g in range(G)]
+        units = (
+            [(g, 0, 0, HALF) for g in range(G)]
+            + [(g, 1, 0, N) for g in range(G)]
+            + [(g, 0, HALF, N) for g in range(G)]
         )
-        steps = [(k, h) for k, (g, m, halves) in enumerate(passes) for h in halves]
 
         def multiply(i, k):
-            g, m, halves = passes[k]
+            g, m, c0, c1 = units[k]
             rows = slice(ROWS * g, ROWS * (g + 1))
-            window = slice(0, N) if halves == (0,) else slice(HALF, HALF + N)
+            window = slice(HALF + c1 - N, HALF + c1)
             nc.tensor.matmul_mx(
                 out=banks[i][g][:],
                 lhsT=words[i][rows, 2 * M_TILE * m : 2 * M_TILE * (m + 1)].bitcast(FP4X4),
-                lhsT_scale=planes[rows, i, M_TILE * m : M_TILE * (m + 1)],
+                lhsT_scale=weight_scales[rows, i, M_TILE * m : M_TILE * (m + 1)],
                 rhs=x_codes[rows, window].bitcast(FP8X4),
                 rhs_scale=x_scales[rows, window],
                 start=True,
                 stop=True,
             )
 
-        def sums(i, k, h):
-            g, m, halves = passes[k]
-            first = HALF if halves == (0,) else h * HALF
-            return banks[i][g][:, first : first + HALF]
+        def sums(i, k):
+            g, m, c0, c1 = units[k]
+            return banks[i][g][:, N - (c1 - c0) : N]
 
         load_x(0)
-        nc.vector.memset(planes[:].rearrange("p i m -> p (i m)").bitcast(I32), 0)
-        nc.vector.memset(warm_in[:], 0.0)
+        nc.vector.memset(weight_scales[:].rearrange("p i m -> p (i m)").bitcast(I32), 0)
         nc.vector.memset(x_codes[:, 0:HALF], 0)
         nc.vector.memset(x_scales[:, 0:HALF].bitcast(I32), 0)
-        load_words(0, w_words)
+        load_words(W)
         for g in range(G):
-            load_scales(g, 0)
-        load_scales(0, 1)
+            load_scales(W, g)
+        load_scales(U, 0)
         load_x(1)
-        load_words(1, u_words)
+        load_words(U)
         for g in range(1, G):
-            load_scales(g, 1)
-        nc.scalar.activation(out=warm_out[:], in_=warm_in[:], func=SILU)
+            load_scales(U, g)
 
-        interleave(nc.vector.tensor_copy, 0, 0, QUARTER)
-        interleave(nc.vector.tensor_copy, 0, QUARTER, HALF - SCALAR_COLS)
-        interleave(nc.scalar.copy, 0, HALF - SCALAR_COLS, HALF)
-        quantize(0, 0)
-        quantize(0, 1)
-        interleave(nc.vector.tensor_copy, 1, 0, QUARTER)
-        interleave(nc.vector.tensor_copy, 1, QUARTER, HALF - SCALAR_COLS)
-        interleave(nc.scalar.copy, 1, HALF - SCALAR_COLS, HALF)
-        quantize(1, 0)
-        quantize(1, 1)
+        for h in range(2):
+            for q in range(2):
+                interleave(h, q)
+            for q in range(2):
+                quantize(h, q)
 
-        for i in range(2):
+        for i in (W, U):
             for k in range(G):
                 multiply(i, k)
 
-        gates = [keep.tile([P, HALF], F32, name=f"gate{s}") for s in range(len(steps))]
-        results = [keep.tile([P, HALF * len(halves)], F32, name=f"result{k}") for k, (g, m, halves) in enumerate(passes)]
+        gates = [keep.tile([P, c1 - c0], F32, name=f"gate{k}") for k, (g, m, c0, c1) in enumerate(units)]
+        results = [keep.tile([P, c1 - c0], F32, name=f"result{k}") for k, (g, m, c0, c1) in enumerate(units)]
 
-        def activate(s):
-            k, h = steps[s]
-            nc.scalar.activation(out=gates[s][:], in_=sums(0, k, h), func=SILU)
-            if h == passes[k][2][-1] and k + G < len(passes):
-                multiply(0, k + G)
+        def activate(k):
+            nc.scalar.activation(out=gates[k][:], in_=sums(W, k), func=SILU)
+            if k + G < len(units):
+                multiply(W, k + G)
 
-        def combine(s):
-            k, h = steps[s]
-            g, m, halves = passes[k]
-            place = (h - halves[0]) * HALF
-            nc.vector.tensor_tensor(out=results[k][:, place : place + HALF], in0=sums(1, k, h), in1=gates[s][:], op=MULT)
-            if h == halves[-1]:
-                nc.sync.dma_start(
-                    out=out[g, M_TILE * m : M_TILE * (m + 1), halves[0] * HALF : (h + 1) * HALF], in_=results[k][:]
-                )
-                if k + G < len(passes):
-                    multiply(1, k + G)
+        def combine(k):
+            g, m, c0, c1 = units[k]
+            nc.vector.tensor_tensor(out=results[k][:], in0=sums(U, k), in1=gates[k][:], op=MULT)
+            nc.sync.dma_start(out=out[g, M_TILE * m : M_TILE * (m + 1), c0:c1], in_=results[k][:])
+            if k + G < len(units):
+                multiply(U, k + G)
 
-        for s in range(len(steps) + 1):
-            if s < len(steps):
-                activate(s)
-            if s >= 1:
-                combine(s - 1)
+        activate(0)
+        for k in range(1, len(units)):
+            activate(k)
+            combine(k - 1)
+        combine(len(units) - 1)

@@ -20,8 +20,10 @@ PACK = 4
 ROWS = D // PACK
 SCALE_ROWS = D // 32
 M_TILE = 128
-HALF = N // 2
-QUARTER = N // 4
+CHUNKS = ((0, 128, 192), (192, 320, 384), (384, 448, 512))
+FIRST = CHUNKS[0][-1]
+PAD = N - FIRST
+STEP = 320
 RUN = 4
 W, U = 0, 1
 
@@ -33,10 +35,10 @@ def tile_rows_gglu_silu_kernel(tc, x, w_words, w_scales, u_words, u_scales, out)
         psum = ctx.enter_context(tc.psum_pool(name="psum", bufs=1))
         ctx.enter_context(tc.manual_schedule())
 
-        raw = [keep.tile([P, PACK, HALF], F32, name=f"raw{h}", align_bytes=64) for h in range(2)]
-        grouped = [keep.tile([P, HALF, PACK], BF16, name=f"grouped{h}", align_bytes=64) for h in range(2)]
-        x_codes = keep.tile([P, HALF + N], U32, align_bytes=64)
-        x_scales = keep.tile([P, HALF + N], U8, align_bytes=64)
+        raw = [keep.tile([P, PACK, c[-1] - c[0]], F32, name=f"raw{h}", align_bytes=64) for h, c in enumerate(CHUNKS)]
+        grouped = keep.tile([P, N, PACK], BF16, align_bytes=64)
+        x_codes = keep.tile([P, PAD + N], U32, align_bytes=64)
+        x_scales = keep.tile([P, PAD + N], U8, align_bytes=64)
         words = [keep.tile([P, 2 * M], U8, name=f"words{i}", align_bytes=64) for i in (W, U)]
         weight_scales = keep.tile([P, 2, M], U8, align_bytes=64)
         banks = [[psum.tile([M_TILE, N], F32, name=f"bank{i}{g}") for g in range(G)] for i in (W, U)]
@@ -44,7 +46,7 @@ def tile_rows_gglu_silu_kernel(tc, x, w_words, w_scales, u_words, u_scales, out)
         x_rows = x.rearrange("g (p j) n -> (g p) j n", j=PACK)
 
         def load_x(h):
-            nc.sync.dma_start(out=raw[h][:], in_=x_rows[:, :, h * HALF : (h + 1) * HALF])
+            nc.sync.dma_start(out=raw[h][:], in_=x_rows[:, :, CHUNKS[h][0] : CHUNKS[h][-1]])
 
         def load_words(i):
             src = (w_words, u_words)[i]
@@ -56,31 +58,36 @@ def tile_rows_gglu_silu_kernel(tc, x, w_words, w_scales, u_words, u_scales, out)
                 out=weight_scales[ROWS * g : ROWS * g + SCALE_ROWS, i, :].bitcast(I32), in_=src[g].bitcast(I32)
             )
 
-        def interleave(h, q):
-            cols = slice(q * QUARTER, (q + 1) * QUARTER)
+        def interleave(h, c0, c1):
             nc.vector.tensor_copy(
-                out=grouped[h][:, cols, :].rearrange("p (c i) j -> p c j i", i=RUN),
-                in_=raw[h][:, :, cols].rearrange("p j (c i) -> p c j i", i=RUN),
+                out=grouped[:, c0:c1, :].rearrange("p (c i) j -> p c j i", i=RUN),
+                in_=raw[h][:, :, c0 - CHUNKS[h][0] : c1 - CHUNKS[h][0]].rearrange("p j (c i) -> p c j i", i=RUN),
             )
 
-        def quantize(h, q):
-            first = (h + 1) * HALF + q * QUARTER
+        def quantize(c0, c1):
             nc.vector.quantize_mx(
-                out=x_codes[:, first : first + QUARTER].bitcast(FP8X4),
-                scales=x_scales[:, first : first + QUARTER],
-                in_=grouped[h][:, q * QUARTER : (q + 1) * QUARTER, :].rearrange("p n j -> p (n j)"),
+                out=x_codes[:, PAD + c0 : PAD + c1].bitcast(FP8X4),
+                scales=x_scales[:, PAD + c0 : PAD + c1],
+                in_=grouped[:, c0:c1, :].rearrange("p n j -> p (n j)"),
             )
+
+        def prepare(h):
+            pieces = list(zip(CHUNKS[h], CHUNKS[h][1:]))
+            for c0, c1 in pieces:
+                interleave(h, c0, c1)
+            for c0, c1 in pieces:
+                quantize(c0, c1)
 
         units = (
-            [(g, 0, 0, HALF) for g in range(G)]
+            [(g, 0, 0, FIRST) for g in range(G)]
             + [(g, 1, 0, N) for g in range(G)]
-            + [(g, 0, HALF, N) for g in range(G)]
+            + [(g, 0, FIRST, N) for g in range(G)]
         )
 
         def multiply(i, k):
             g, m, c0, c1 = units[k]
             rows = slice(ROWS * g, ROWS * (g + 1))
-            window = slice(HALF + c1 - N, HALF + c1)
+            window = slice(PAD + c1 - N, PAD + c1)
             nc.tensor.matmul_mx(
                 out=banks[i][g][:],
                 lhsT=words[i][rows, 2 * M_TILE * m : 2 * M_TILE * (m + 1)].bitcast(FP4X4),
@@ -91,44 +98,50 @@ def tile_rows_gglu_silu_kernel(tc, x, w_words, w_scales, u_words, u_scales, out)
                 stop=True,
             )
 
-        def sums(i, k):
+        def steps(k):
+            width = units[k][3] - units[k][2]
+            count = -(-width // STEP)
+            return [slice(s * width // count, (s + 1) * width // count) for s in range(count)]
+
+        def sums(i, k, cols):
             g, m, c0, c1 = units[k]
-            return banks[i][g][:, N - (c1 - c0) : N]
+            return banks[i][g][:, N - (c1 - c0) : N][:, cols]
 
         load_x(0)
         nc.vector.memset(weight_scales[:].rearrange("p i m -> p (i m)").bitcast(I32), 0)
-        nc.vector.memset(x_codes[:, 0:HALF], 0)
-        nc.vector.memset(x_scales[:, 0:HALF].bitcast(I32), 0)
-        load_words(W)
-        for g in range(G):
-            load_scales(W, g)
-        load_scales(U, 0)
-        load_x(1)
-        load_words(U)
-        for g in range(1, G):
-            load_scales(U, g)
-
-        for h in range(2):
-            for q in range(2):
-                interleave(h, q)
-            for q in range(2):
-                quantize(h, q)
-
+        nc.vector.memset(x_codes[:, 0:PAD], 0)
+        nc.vector.memset(x_scales[:, 0:PAD].bitcast(I32), 0)
         for i in (W, U):
-            for k in range(G):
-                multiply(i, k)
+            load_words(i)
+            for g in range(G // 2):
+                load_scales(i, g)
+        load_x(1)
+        load_x(2)
+        for i in (W, U):
+            for g in range(G // 2, G):
+                load_scales(i, g)
+
+        for h in range(len(CHUNKS)):
+            prepare(h)
+
+        for first in (0, G // 2):
+            for i in (W, U):
+                for k in range(first, first + G // 2):
+                    multiply(i, k)
 
         gates = [keep.tile([P, c1 - c0], F32, name=f"gate{k}") for k, (g, m, c0, c1) in enumerate(units)]
         results = [keep.tile([P, c1 - c0], F32, name=f"result{k}") for k, (g, m, c0, c1) in enumerate(units)]
 
         def activate(k):
-            nc.scalar.activation(out=gates[k][:], in_=sums(W, k), func=SILU)
+            for cols in steps(k):
+                nc.scalar.activation(out=gates[k][:, cols], in_=sums(W, k, cols), func=SILU)
             if k + G < len(units):
                 multiply(W, k + G)
 
         def combine(k):
             g, m, c0, c1 = units[k]
-            nc.vector.tensor_tensor(out=results[k][:], in0=sums(U, k), in1=gates[k][:], op=MULT)
+            for cols in steps(k):
+                nc.vector.tensor_tensor(out=results[k][:, cols], in0=sums(U, k, cols), in1=gates[k][:, cols], op=MULT)
             nc.sync.dma_start(out=out[g, M_TILE * m : M_TILE * (m + 1), c0:c1], in_=results[k][:])
             if k + G < len(units):
                 multiply(U, k + G)

@@ -20,10 +20,10 @@ PACK = 4
 ROWS = D // PACK
 SCALE_ROWS = D // 32
 M_TILE = 128
-CHUNKS = ((0, 128, 192), (192, 320, 384), (384, 448, 512))
+CHUNKS = ((0, 128, 256), (256, 384, 512))
 FIRST = CHUNKS[0][-1]
 PAD = N - FIRST
-STEP = 320
+STEP = 256
 RUN = 4
 W, U = 0, 1
 
@@ -116,7 +116,6 @@ def tile_rows_gglu_silu_kernel(tc, x, w_words, w_scales, u_words, u_scales, out)
             for g in range(G // 2):
                 load_scales(i, g)
         load_x(1)
-        load_x(2)
         for i in (W, U):
             for g in range(G // 2, G):
                 load_scales(i, g)

@@ -23,7 +23,7 @@ M_TILE = 128
 CHUNKS = ((0, 128, 256), (256, 384, 512))
 FIRST = CHUNKS[0][-1]
 PAD = N - FIRST
-STEP = 256
+STEP = 512
 RUN = 4
 W, U = 0, 1
 
@@ -107,26 +107,25 @@ def tile_rows_gglu_silu_kernel(tc, x, w_words, w_scales, u_words, u_scales, out)
             g, m, c0, c1 = units[k]
             return banks[i][g][:, N - (c1 - c0) : N][:, cols]
 
+        in_front = [(W, 0), (W, 1), (W, 2), (U, 0)]
+        behind = [(W, 3), (U, 1), (U, 2), (U, 3)]
         load_x(0)
         nc.vector.memset(weight_scales[:].rearrange("p i m -> p (i m)").bitcast(I32), 0)
         nc.vector.memset(x_codes[:, 0:PAD], 0)
         nc.vector.memset(x_scales[:, 0:PAD].bitcast(I32), 0)
-        for i in (W, U):
-            load_words(i)
-            for g in range(G // 2):
-                load_scales(i, g)
+        for i, g in in_front:
+            if g == 0:
+                load_words(i)
+            load_scales(i, g)
         load_x(1)
-        for i in (W, U):
-            for g in range(G // 2, G):
-                load_scales(i, g)
+        for i, g in behind:
+            load_scales(i, g)
 
         for h in range(len(CHUNKS)):
             prepare(h)
 
-        for first in (0, G // 2):
-            for i in (W, U):
-                for k in range(first, first + G // 2):
-                    multiply(i, k)
+        for i, g in in_front + behind:
+            multiply(i, g)
 
         gates = [keep.tile([P, c1 - c0], F32, name=f"gate{k}") for k, (g, m, c0, c1) in enumerate(units)]
         results = [keep.tile([P, c1 - c0], F32, name=f"result{k}") for k, (g, m, c0, c1) in enumerate(units)]

@@ -24,6 +24,7 @@ CHUNKS = ((0, 128, 256), (256, 384, 512))
 FIRST = CHUNKS[0][-1]
 PAD = N - FIRST
 STEP = 512
+SHARE = 64
 RUN = 4
 W, U = 0, 1
 
@@ -39,7 +40,10 @@ def tile_rows_gglu_silu_kernel(tc, x, w_words, w_scales, u_words, u_scales, out)
         grouped = keep.tile([P, N, PACK], BF16, align_bytes=64)
         x_codes = keep.tile([P, PAD + N], U32, align_bytes=64)
         x_scales = keep.tile([P, PAD + N], U8, align_bytes=64)
-        words = [keep.tile([P, 2 * M], U8, name=f"words{i}", align_bytes=64) for i in (W, U)]
+        words = [
+            [keep.tile([P, 2 * M_TILE], U8, name=f"words{i}{m}", align_bytes=64) for m in range(M // M_TILE)]
+            for i in (W, U)
+        ]
         weight_scales = keep.tile([P, 2, M], U8, align_bytes=64)
         banks = [[psum.tile([M_TILE, N], F32, name=f"bank{i}{g}") for g in range(G)] for i in (W, U)]
 
@@ -48,9 +52,9 @@ def tile_rows_gglu_silu_kernel(tc, x, w_words, w_scales, u_words, u_scales, out)
         def load_x(h):
             nc.sync.dma_start(out=raw[h][:], in_=x_rows[:, :, CHUNKS[h][0] : CHUNKS[h][-1]])
 
-        def load_words(i):
-            src = (w_words, u_words)[i]
-            nc.sync.dma_start(out=words[i][:].bitcast(I32), in_=src.rearrange("g p b -> (g p) b").bitcast(I32))
+        def load_words(i, m):
+            src = (w_words, u_words)[i].rearrange("g p b -> (g p) b")[:, 2 * M_TILE * m : 2 * M_TILE * (m + 1)]
+            nc.sync.dma_start(out=words[i][m][:].bitcast(I32), in_=src.bitcast(I32))
 
         def load_scales(i, g):
             src = (w_scales, u_scales)[i]
@@ -58,8 +62,8 @@ def tile_rows_gglu_silu_kernel(tc, x, w_words, w_scales, u_words, u_scales, out)
                 out=weight_scales[ROWS * g : ROWS * g + SCALE_ROWS, i, :].bitcast(I32), in_=src[g].bitcast(I32)
             )
 
-        def interleave(h, c0, c1):
-            nc.vector.tensor_copy(
+        def interleave(copy, h, c0, c1):
+            copy(
                 out=grouped[:, c0:c1, :].rearrange("p (c i) j -> p c j i", i=RUN),
                 in_=raw[h][:, :, c0 - CHUNKS[h][0] : c1 - CHUNKS[h][0]].rearrange("p j (c i) -> p c j i", i=RUN),
             )
@@ -73,8 +77,10 @@ def tile_rows_gglu_silu_kernel(tc, x, w_words, w_scales, u_words, u_scales, out)
 
         def prepare(h):
             pieces = list(zip(CHUNKS[h], CHUNKS[h][1:]))
+            shared = CHUNKS[h][-1] - SHARE
+            interleave(nc.scalar.copy, h, shared, CHUNKS[h][-1])
             for c0, c1 in pieces:
-                interleave(h, c0, c1)
+                interleave(nc.vector.tensor_copy, h, c0, min(c1, shared))
             for c0, c1 in pieces:
                 quantize(c0, c1)
 
@@ -90,7 +96,7 @@ def tile_rows_gglu_silu_kernel(tc, x, w_words, w_scales, u_words, u_scales, out)
             window = slice(PAD + c1 - N, PAD + c1)
             nc.tensor.matmul_mx(
                 out=banks[i][g][:],
-                lhsT=words[i][rows, 2 * M_TILE * m : 2 * M_TILE * (m + 1)].bitcast(FP4X4),
+                lhsT=words[i][m][rows, :].bitcast(FP4X4),
                 lhsT_scale=weight_scales[rows, i, M_TILE * m : M_TILE * (m + 1)],
                 rhs=x_codes[rows, window].bitcast(FP8X4),
                 rhs_scale=x_scales[rows, window],
@@ -107,19 +113,23 @@ def tile_rows_gglu_silu_kernel(tc, x, w_words, w_scales, u_words, u_scales, out)
             g, m, c0, c1 = units[k]
             return banks[i][g][:, N - (c1 - c0) : N][:, cols]
 
-        in_front = [(W, 0), (W, 1), (W, 2), (U, 0)]
-        behind = [(W, 3), (U, 1), (U, 2), (U, 3)]
+        in_front = [(W, 0), (W, 1), (U, 0), (W, 2)]
+        behind = [(U, 1), (W, 3), (U, 2), (U, 3)]
         load_x(0)
         nc.vector.memset(weight_scales[:].rearrange("p i m -> p (i m)").bitcast(I32), 0)
         nc.vector.memset(x_codes[:, 0:PAD], 0)
         nc.vector.memset(x_scales[:, 0:PAD].bitcast(I32), 0)
+        warm = keep.tile([P, 1], F32)
+        nc.scalar.activation(out=warm[:], in_=x_codes[:, 0:1].bitcast(F32), func=SILU)
         for i, g in in_front:
             if g == 0:
-                load_words(i)
+                load_words(i, 0)
             load_scales(i, g)
         load_x(1)
         for i, g in behind:
             load_scales(i, g)
+        for i in (W, U):
+            load_words(i, 1)
 
         for h in range(len(CHUNKS)):
             prepare(h)
@@ -128,7 +138,10 @@ def tile_rows_gglu_silu_kernel(tc, x, w_words, w_scales, u_words, u_scales, out)
             multiply(i, g)
 
         gates = [keep.tile([P, c1 - c0], F32, name=f"gate{k}") for k, (g, m, c0, c1) in enumerate(units)]
-        results = [keep.tile([P, c1 - c0], F32, name=f"result{k}") for k, (g, m, c0, c1) in enumerate(units)]
+        pairs = [keep.tile([P, 2, FIRST], F32, name=f"pair{k}") for k in range(G // 2)]
+        results = [pairs[k // 2][:, k % 2, :] for k in range(G)] + [
+            keep.tile([P, c1 - c0], F32, name=f"result{k}")[:] for k, (g, m, c0, c1) in enumerate(units[G:])
+        ]
 
         def activate(k):
             for cols in steps(k):
@@ -140,7 +153,11 @@ def tile_rows_gglu_silu_kernel(tc, x, w_words, w_scales, u_words, u_scales, out)
             g, m, c0, c1 = units[k]
             for cols in steps(k):
                 nc.vector.tensor_tensor(out=results[k][:, cols], in0=sums(U, k, cols), in1=gates[k][:, cols], op=MULT)
-            nc.sync.dma_start(out=out[g, M_TILE * m : M_TILE * (m + 1), c0:c1], in_=results[k][:])
+            if k >= G:
+                nc.sync.dma_start(out=out[g, M_TILE * m : M_TILE * (m + 1), c0:c1], in_=results[k])
+            elif k % 2 == 1:
+                both = out[g - 1 : g + 1, 0:M_TILE, c0:c1].rearrange("g m n -> m g n")
+                nc.sync.dma_start(out=both, in_=pairs[k // 2][:])
             if k + G < len(units):
                 multiply(U, k + G)
 

@@ -23,7 +23,7 @@ M_TILE = 128
 CHUNKS = ((0, 128, 256), (256, 384, 512))
 FIRST = CHUNKS[0][-1]
 PAD = N - FIRST
-STEP = 512
+STEP = 256
 SHARE = 64
 RUN = 4
 W, U = 0, 1
@@ -138,10 +138,16 @@ def tile_rows_gglu_silu_kernel(tc, x, w_words, w_scales, u_words, u_scales, out)
             multiply(i, g)
 
         gates = [keep.tile([P, c1 - c0], F32, name=f"gate{k}") for k, (g, m, c0, c1) in enumerate(units)]
-        pairs = [keep.tile([P, 2, FIRST], F32, name=f"pair{k}") for k in range(G // 2)]
-        results = [pairs[k // 2][:, k % 2, :] for k in range(G)] + [
-            keep.tile([P, c1 - c0], F32, name=f"result{k}")[:] for k, (g, m, c0, c1) in enumerate(units[G:])
-        ]
+        paired = (G - 2, 2 * G)
+        stores = [[k, k + 1] if k in paired else [k] for k in range(len(units)) if k - 1 not in paired]
+        leaving, results = {}, {}
+        for members in stores:
+            g, m, c0, c1 = units[members[0]]
+            tile = keep.tile([P, len(members), c1 - c0], F32, name=f"result{members[0]}")
+            for place, k in enumerate(members):
+                results.setdefault(k, tile[:, place, :])
+            rows = out[g : g + len(members), M_TILE * m : M_TILE * (m + 1), c0:c1].rearrange("g m n -> m g n")
+            leaving.setdefault(members[-1], (rows, tile))
 
         def activate(k):
             for cols in steps(k):
@@ -150,14 +156,10 @@ def tile_rows_gglu_silu_kernel(tc, x, w_words, w_scales, u_words, u_scales, out)
                 multiply(W, k + G)
 
         def combine(k):
-            g, m, c0, c1 = units[k]
             for cols in steps(k):
                 nc.vector.tensor_tensor(out=results[k][:, cols], in0=sums(U, k, cols), in1=gates[k][:, cols], op=MULT)
-            if k >= G:
-                nc.sync.dma_start(out=out[g, M_TILE * m : M_TILE * (m + 1), c0:c1], in_=results[k])
-            elif k % 2 == 1:
-                both = out[g - 1 : g + 1, 0:M_TILE, c0:c1].rearrange("g m n -> m g n")
-                nc.sync.dma_start(out=both, in_=pairs[k // 2][:])
+            if k in leaving:
+                nc.sync.dma_start(out=leaving[k][0], in_=leaving[k][1][:])
             if k + G < len(units):
                 multiply(U, k + G)
 

@@ -24,7 +24,6 @@ CHUNKS = ((0, 128, 256), (256, 384, 512))
 FIRST = CHUNKS[0][-1]
 PAD = N - FIRST
 STEP = 256
-SHARE = 64
 RUN = 4
 W, U = 0, 1
 
@@ -62,8 +61,8 @@ def tile_rows_gglu_silu_kernel(tc, x, w_words, w_scales, u_words, u_scales, out)
                 out=weight_scales[ROWS * g : ROWS * g + SCALE_ROWS, i, :].bitcast(I32), in_=src[g].bitcast(I32)
             )
 
-        def interleave(copy, h, c0, c1):
-            copy(
+        def interleave(h, c0, c1):
+            nc.vector.tensor_copy(
                 out=grouped[:, c0:c1, :].rearrange("p (c i) j -> p c j i", i=RUN),
                 in_=raw[h][:, :, c0 - CHUNKS[h][0] : c1 - CHUNKS[h][0]].rearrange("p j (c i) -> p c j i", i=RUN),
             )
@@ -77,10 +76,8 @@ def tile_rows_gglu_silu_kernel(tc, x, w_words, w_scales, u_words, u_scales, out)
 
         def prepare(h):
             pieces = list(zip(CHUNKS[h], CHUNKS[h][1:]))
-            shared = CHUNKS[h][-1] - SHARE
-            interleave(nc.scalar.copy, h, shared, CHUNKS[h][-1])
             for c0, c1 in pieces:
-                interleave(nc.vector.tensor_copy, h, c0, min(c1, shared))
+                interleave(h, c0, c1)
             for c0, c1 in pieces:
                 quantize(c0, c1)
 
@@ -119,8 +116,6 @@ def tile_rows_gglu_silu_kernel(tc, x, w_words, w_scales, u_words, u_scales, out)
         nc.vector.memset(weight_scales[:].rearrange("p i m -> p (i m)").bitcast(I32), 0)
         nc.vector.memset(x_codes[:, 0:PAD], 0)
         nc.vector.memset(x_scales[:, 0:PAD].bitcast(I32), 0)
-        warm = keep.tile([P, 1], F32)
-        nc.scalar.activation(out=warm[:], in_=x_codes[:, 0:1].bitcast(F32), func=SILU)
         for i, g in in_front:
             if g == 0:
                 load_words(i, 0)

@@ -39,9 +39,11 @@ def tile_rows_gglu_silu_kernel(tc, x, w_words, w_scales, u_words, u_scales, out)
         grouped = keep.tile([P, N, PACK], BF16, align_bytes=64)
         x_codes = keep.tile([P, PAD + N], U32, align_bytes=64)
         x_scales = keep.tile([P, PAD + N], U8, align_bytes=64)
+        w_tiles = [keep.tile([P, 2 * M_TILE], U8, name=f"w_tile{m}", align_bytes=64) for m in range(M // M_TILE)]
+        u_tile = keep.tile([P, 2 * M], U8, align_bytes=64)
         words = [
-            [keep.tile([P, 2 * M_TILE], U8, name=f"words{i}{m}", align_bytes=64) for m in range(M // M_TILE)]
-            for i in (W, U)
+            [tile[:] for tile in w_tiles],
+            [u_tile[:, 2 * M_TILE * m : 2 * M_TILE * (m + 1)] for m in range(M // M_TILE)],
         ]
         weight_scales = keep.tile([P, 2, M], U8, align_bytes=64)
         banks = [[psum.tile([M_TILE, N], F32, name=f"bank{i}{g}") for g in range(G)] for i in (W, U)]
@@ -51,9 +53,9 @@ def tile_rows_gglu_silu_kernel(tc, x, w_words, w_scales, u_words, u_scales, out)
         def load_x(h):
             nc.sync.dma_start(out=raw[h][:], in_=x_rows[:, :, CHUNKS[h][0] : CHUNKS[h][-1]])
 
-        def load_words(i, m):
-            src = (w_words, u_words)[i].rearrange("g p b -> (g p) b")[:, 2 * M_TILE * m : 2 * M_TILE * (m + 1)]
-            nc.sync.dma_start(out=words[i][m][:].bitcast(I32), in_=src.bitcast(I32))
+        def load_words(tile, src, first_byte):
+            rows = src.rearrange("g p b -> (g p) b")[:, first_byte : first_byte + tile.shape[1]]
+            nc.sync.dma_start(out=tile[:].bitcast(I32), in_=rows.bitcast(I32))
 
         def load_scales(i, g):
             src = (w_scales, u_scales)[i]
@@ -110,39 +112,44 @@ def tile_rows_gglu_silu_kernel(tc, x, w_words, w_scales, u_words, u_scales, out)
             g, m, c0, c1 = units[k]
             return banks[i][g][:, N - (c1 - c0) : N][:, cols]
 
-        in_front = [(W, 0), (W, 1), (U, 0), (W, 2)]
-        behind = [(U, 1), (W, 3), (U, 2), (U, 3)]
         load_x(0)
         nc.vector.memset(weight_scales[:].rearrange("p i m -> p (i m)").bitcast(I32), 0)
         nc.vector.memset(x_codes[:, 0:PAD], 0)
         nc.vector.memset(x_scales[:, 0:PAD].bitcast(I32), 0)
-        for i, g in in_front:
-            if g == 0:
-                load_words(i, 0)
-            load_scales(i, g)
+        load_words(w_tiles[0], w_words, 0)
+        for g in range(G):
+            load_scales(W, g)
         load_x(1)
-        for i, g in behind:
-            load_scales(i, g)
-        for i in (W, U):
-            load_words(i, 1)
+        load_words(u_tile, u_words, 0)
+        for g in range(G):
+            load_scales(U, g)
+        load_words(w_tiles[1], w_words, 2 * M_TILE)
 
         for h in range(len(CHUNKS)):
             prepare(h)
 
-        for i, g in in_front + behind:
-            multiply(i, g)
+        for i in (W, U):
+            for g in range(G):
+                multiply(i, g)
 
         gates = [keep.tile([P, c1 - c0], F32, name=f"gate{k}") for k, (g, m, c0, c1) in enumerate(units)]
-        paired = (G - 2, 2 * G)
-        stores = [[k, k + 1] if k in paired else [k] for k in range(len(units)) if k - 1 not in paired]
-        leaving, results = {}, {}
-        for members in stores:
-            g, m, c0, c1 = units[members[0]]
-            tile = keep.tile([P, len(members), c1 - c0], F32, name=f"result{members[0]}")
-            for place, k in enumerate(members):
-                results.setdefault(k, tile[:, place, :])
-            rows = out[g : g + len(members), M_TILE * m : M_TILE * (m + 1), c0:c1].rearrange("g m n -> m g n")
-            leaving.setdefault(members[-1], (rows, tile))
+        paired = (0, 2)
+        by_step = (G,)
+        results, pair_tiles = {}, {}
+        for k, (g, m, c0, c1) in enumerate(units):
+            if k - 1 in paired:
+                continue
+            count = 2 if k in paired else 1
+            tile = keep.tile([P, count, c1 - c0], F32, name=f"result{k}")
+            for place in range(count):
+                results.setdefault(k + place, tile[:, place, :])
+            pair_tiles.setdefault(k + count - 1, (k, tile))
+
+        def store(k, cols):
+            first, tile = pair_tiles[k]
+            g, m, c0, c1 = units[first]
+            rows = out[g : g + k - first + 1, M_TILE * m : M_TILE * (m + 1), c0:c1].rearrange("g m n -> m g n")
+            nc.sync.dma_start(out=rows[:, :, cols], in_=tile[:, :, cols])
 
         def activate(k):
             for cols in steps(k):
@@ -153,8 +160,10 @@ def tile_rows_gglu_silu_kernel(tc, x, w_words, w_scales, u_words, u_scales, out)
         def combine(k):
             for cols in steps(k):
                 nc.vector.tensor_tensor(out=results[k][:, cols], in0=sums(U, k, cols), in1=gates[k][:, cols], op=MULT)
-            if k in leaving:
-                nc.sync.dma_start(out=leaving[k][0], in_=leaving[k][1][:])
+                if k in by_step:
+                    store(k, cols)
+            if k in pair_tiles and k not in by_step:
+                store(k, slice(None))
             if k + G < len(units):
                 multiply(U, k + G)
 

@@ -25,6 +25,7 @@ FIRST = CHUNKS[0][-1]
 PAD = N - FIRST
 STEP = 256
 RUN = 4
+PAIR = 2
 W, U = 0, 1
 
 
@@ -35,7 +36,10 @@ def tile_rows_gglu_silu_kernel(tc, x, w_words, w_scales, u_words, u_scales, out)
         psum = ctx.enter_context(tc.psum_pool(name="psum", bufs=1))
         ctx.enter_context(tc.manual_schedule())
 
-        raw = [keep.tile([P, PACK, c[-1] - c[0]], F32, name=f"raw{h}", align_bytes=64) for h, c in enumerate(CHUNKS)]
+        raw = [
+            [keep.tile([P, PAIR, c[-1] - c[0]], F32, name=f"raw{h}{j}", align_bytes=64) for j in range(PACK // PAIR)]
+            for h, c in enumerate(CHUNKS)
+        ]
         grouped = keep.tile([P, N, PACK], BF16, align_bytes=64)
         x_codes = keep.tile([P, PAD + N], U32, align_bytes=64)
         x_scales = keep.tile([P, PAD + N], U8, align_bytes=64)
@@ -51,7 +55,8 @@ def tile_rows_gglu_silu_kernel(tc, x, w_words, w_scales, u_words, u_scales, out)
         x_rows = x.rearrange("g (p j) n -> (g p) j n", j=PACK)
 
         def load_x(h):
-            nc.sync.dma_start(out=raw[h][:], in_=x_rows[:, :, CHUNKS[h][0] : CHUNKS[h][-1]])
+            for j, tile in enumerate(raw[h]):
+                nc.sync.dma_start(out=tile[:], in_=x_rows[:, PAIR * j : PAIR * (j + 1), CHUNKS[h][0] : CHUNKS[h][-1]])
 
         def load_words(tile, src, first_byte):
             rows = src.rearrange("g p b -> (g p) b")[:, first_byte : first_byte + tile.shape[1]]
@@ -63,10 +68,10 @@ def tile_rows_gglu_silu_kernel(tc, x, w_words, w_scales, u_words, u_scales, out)
                 out=weight_scales[ROWS * g : ROWS * g + SCALE_ROWS, i, :].bitcast(I32), in_=src[g].bitcast(I32)
             )
 
-        def interleave(h, c0, c1):
+        def interleave(h, j, c0, c1):
             nc.vector.tensor_copy(
-                out=grouped[:, c0:c1, :].rearrange("p (c i) j -> p c j i", i=RUN),
-                in_=raw[h][:, :, c0 - CHUNKS[h][0] : c1 - CHUNKS[h][0]].rearrange("p j (c i) -> p c j i", i=RUN),
+                out=grouped[:, c0:c1, PAIR * j : PAIR * (j + 1)].rearrange("p (c i) j -> p c j i", i=RUN),
+                in_=raw[h][j][:, :, c0 - CHUNKS[h][0] : c1 - CHUNKS[h][0]].rearrange("p j (c i) -> p c j i", i=RUN),
             )
 
         def quantize(c0, c1):
@@ -78,8 +83,9 @@ def tile_rows_gglu_silu_kernel(tc, x, w_words, w_scales, u_words, u_scales, out)
 
         def prepare(h):
             pieces = list(zip(CHUNKS[h], CHUNKS[h][1:]))
+            interleave(h, 0, CHUNKS[h][0], CHUNKS[h][-1])
             for c0, c1 in pieces:
-                interleave(h, c0, c1)
+                interleave(h, 1, c0, c1)
             for c0, c1 in pieces:
                 quantize(c0, c1)
 
@@ -117,9 +123,10 @@ def tile_rows_gglu_silu_kernel(tc, x, w_words, w_scales, u_words, u_scales, out)
         nc.vector.memset(x_codes[:, 0:PAD], 0)
         nc.vector.memset(x_scales[:, 0:PAD].bitcast(I32), 0)
         load_words(w_tiles[0], w_words, 0)
-        for g in range(G):
+        for g in range(G - 1):
             load_scales(W, g)
         load_x(1)
+        load_scales(W, G - 1)
         load_words(u_tile, u_words, 0)
         for g in range(G):
             load_scales(U, g)
@@ -133,8 +140,7 @@ def tile_rows_gglu_silu_kernel(tc, x, w_words, w_scales, u_words, u_scales, out)
                 multiply(i, g)
 
         gates = [keep.tile([P, c1 - c0], F32, name=f"gate{k}") for k, (g, m, c0, c1) in enumerate(units)]
-        paired = (0, 2)
-        by_step = (G,)
+        paired = (0, 2, 2 * G)
         results, pair_tiles = {}, {}
         for k, (g, m, c0, c1) in enumerate(units):
             if k - 1 in paired:
@@ -145,11 +151,11 @@ def tile_rows_gglu_silu_kernel(tc, x, w_words, w_scales, u_words, u_scales, out)
                 results.setdefault(k + place, tile[:, place, :])
             pair_tiles.setdefault(k + count - 1, (k, tile))
 
-        def store(k, cols):
+        def store(k):
             first, tile = pair_tiles[k]
             g, m, c0, c1 = units[first]
             rows = out[g : g + k - first + 1, M_TILE * m : M_TILE * (m + 1), c0:c1].rearrange("g m n -> m g n")
-            nc.sync.dma_start(out=rows[:, :, cols], in_=tile[:, :, cols])
+            nc.sync.dma_start(out=rows, in_=tile[:])
 
         def activate(k):
             for cols in steps(k):
@@ -160,10 +166,8 @@ def tile_rows_gglu_silu_kernel(tc, x, w_words, w_scales, u_words, u_scales, out)
         def combine(k):
             for cols in steps(k):
                 nc.vector.tensor_tensor(out=results[k][:, cols], in0=sums(U, k, cols), in1=gates[k][:, cols], op=MULT)
-                if k in by_step:
-                    store(k, cols)
-            if k in pair_tiles and k not in by_step:
-                store(k, slice(None))
+            if k in pair_tiles:
+                store(k)
             if k + G < len(units):
                 multiply(U, k + G)
 

@@ -43,12 +43,7 @@ def tile_rows_gglu_silu_kernel(tc, x, w_words, w_scales, u_words, u_scales, out)
         grouped = keep.tile([P, N, PACK], BF16, align_bytes=64)
         x_codes = keep.tile([P, PAD + N], U32, align_bytes=64)
         x_scales = keep.tile([P, PAD + N], U8, align_bytes=64)
-        w_tiles = [keep.tile([P, 2 * M_TILE], U8, name=f"w_tile{m}", align_bytes=64) for m in range(M // M_TILE)]
-        u_tile = keep.tile([P, 2 * M], U8, align_bytes=64)
-        words = [
-            [tile[:] for tile in w_tiles],
-            [u_tile[:, 2 * M_TILE * m : 2 * M_TILE * (m + 1)] for m in range(M // M_TILE)],
-        ]
+        words = [keep.tile([P, 2 * M], U8, name=f"words{i}", align_bytes=64) for i in (W, U)]
         weight_scales = keep.tile([P, 2, M], U8, align_bytes=64)
         banks = [[psum.tile([M_TILE, N], F32, name=f"bank{i}{g}") for g in range(G)] for i in (W, U)]
 
@@ -58,9 +53,9 @@ def tile_rows_gglu_silu_kernel(tc, x, w_words, w_scales, u_words, u_scales, out)
             for j, tile in enumerate(raw[h]):
                 nc.sync.dma_start(out=tile[:], in_=x_rows[:, PAIR * j : PAIR * (j + 1), CHUNKS[h][0] : CHUNKS[h][-1]])
 
-        def load_words(tile, src, first_byte):
-            rows = src.rearrange("g p b -> (g p) b")[:, first_byte : first_byte + tile.shape[1]]
-            nc.sync.dma_start(out=tile[:].bitcast(I32), in_=rows.bitcast(I32))
+        def load_words(i):
+            src = (w_words, u_words)[i].rearrange("g p b -> (g p) b")
+            nc.sync.dma_start(out=words[i][:].bitcast(I32), in_=src.bitcast(I32))
 
         def load_scales(i, g):
             src = (w_scales, u_scales)[i]
@@ -89,11 +84,10 @@ def tile_rows_gglu_silu_kernel(tc, x, w_words, w_scales, u_words, u_scales, out)
             for c0, c1 in pieces:
                 quantize(c0, c1)
 
-        units = (
-            [(g, 0, 0, FIRST) for g in range(G)]
-            + [(g, 1, 0, N) for g in range(G)]
-            + [(g, 0, FIRST, N) for g in range(G)]
-        )
+        early = [(g, 0, 0, FIRST) for g in range(G)]
+        late = [(g, 0, FIRST, N) for g in range(G)]
+        whole = [(g, 1, 0, N) for g in range(G)]
+        units = early + late[:-1] + whole[-1:] + whole[:-1] + late[-1:]
 
         def multiply(i, k):
             g, m, c0, c1 = units[k]
@@ -101,7 +95,7 @@ def tile_rows_gglu_silu_kernel(tc, x, w_words, w_scales, u_words, u_scales, out)
             window = slice(PAD + c1 - N, PAD + c1)
             nc.tensor.matmul_mx(
                 out=banks[i][g][:],
-                lhsT=words[i][m][rows, :].bitcast(FP4X4),
+                lhsT=words[i][rows, 2 * M_TILE * m : 2 * M_TILE * (m + 1)].bitcast(FP4X4),
                 lhsT_scale=weight_scales[rows, i, M_TILE * m : M_TILE * (m + 1)],
                 rhs=x_codes[rows, window].bitcast(FP8X4),
                 rhs_scale=x_scales[rows, window],
@@ -122,15 +116,14 @@ def tile_rows_gglu_silu_kernel(tc, x, w_words, w_scales, u_words, u_scales, out)
         nc.vector.memset(weight_scales[:].rearrange("p i m -> p (i m)").bitcast(I32), 0)
         nc.vector.memset(x_codes[:, 0:PAD], 0)
         nc.vector.memset(x_scales[:, 0:PAD].bitcast(I32), 0)
-        load_words(w_tiles[0], w_words, 0)
+        load_words(W)
         for g in range(G - 1):
             load_scales(W, g)
         load_x(1)
         load_scales(W, G - 1)
-        load_words(u_tile, u_words, 0)
+        load_words(U)
         for g in range(G):
             load_scales(U, g)
-        load_words(w_tiles[1], w_words, 2 * M_TILE)
 
         for h in range(len(CHUNKS)):
             prepare(h)
@@ -140,7 +133,7 @@ def tile_rows_gglu_silu_kernel(tc, x, w_words, w_scales, u_words, u_scales, out)
                 multiply(i, g)
 
         gates = [keep.tile([P, c1 - c0], F32, name=f"gate{k}") for k, (g, m, c0, c1) in enumerate(units)]
-        paired = (0, 2, 2 * G)
+        paired = (0, 2)
         results, pair_tiles = {}, {}
         for k, (g, m, c0, c1) in enumerate(units):
             if k - 1 in paired:

@@ -43,7 +43,10 @@ def tile_rows_gglu_silu_kernel(tc, x, w_words, w_scales, u_words, u_scales, out)
         grouped = keep.tile([P, N, PACK], BF16, align_bytes=64)
         x_codes = keep.tile([P, PAD + N], U32, align_bytes=64)
         x_scales = keep.tile([P, PAD + N], U8, align_bytes=64)
-        words = [keep.tile([P, 2 * M], U8, name=f"words{i}", align_bytes=64) for i in (W, U)]
+        words = [
+            [keep.tile([P, 2 * M_TILE], U8, name=f"words{i}{m}", align_bytes=64) for m in range(M // M_TILE)]
+            for i in (W, U)
+        ]
         weight_scales = keep.tile([P, 2, M], U8, align_bytes=64)
         banks = [[psum.tile([M_TILE, N], F32, name=f"bank{i}{g}") for g in range(G)] for i in (W, U)]
 
@@ -53,15 +56,14 @@ def tile_rows_gglu_silu_kernel(tc, x, w_words, w_scales, u_words, u_scales, out)
             for j, tile in enumerate(raw[h]):
                 nc.sync.dma_start(out=tile[:], in_=x_rows[:, PAIR * j : PAIR * (j + 1), CHUNKS[h][0] : CHUNKS[h][-1]])
 
-        def load_words(i):
-            src = (w_words, u_words)[i].rearrange("g p b -> (g p) b")
-            nc.sync.dma_start(out=words[i][:].bitcast(I32), in_=src.bitcast(I32))
+        def load_words(i, m):
+            src = (w_words, u_words)[i].rearrange("g p b -> (g p) b")[:, 2 * M_TILE * m : 2 * M_TILE * (m + 1)]
+            nc.sync.dma_start(out=words[i][m][:].bitcast(I32), in_=src.bitcast(I32))
 
-        def load_scales(i, g):
-            src = (w_scales, u_scales)[i]
-            nc.sync.dma_start(
-                out=weight_scales[ROWS * g : ROWS * g + SCALE_ROWS, i, :].bitcast(I32), in_=src[g].bitcast(I32)
-            )
+        def load_scales(i, g, outputs):
+            src = (w_scales, u_scales)[i][g][:, outputs]
+            rows = slice(ROWS * g, ROWS * g + SCALE_ROWS)
+            nc.sync.dma_start(out=weight_scales[rows, i, outputs].bitcast(I32), in_=src.bitcast(I32))
 
         def interleave(h, j, c0, c1):
             nc.vector.tensor_copy(
@@ -95,7 +97,7 @@ def tile_rows_gglu_silu_kernel(tc, x, w_words, w_scales, u_words, u_scales, out)
             window = slice(PAD + c1 - N, PAD + c1)
             nc.tensor.matmul_mx(
                 out=banks[i][g][:],
-                lhsT=words[i][rows, 2 * M_TILE * m : 2 * M_TILE * (m + 1)].bitcast(FP4X4),
+                lhsT=words[i][m][rows, :].bitcast(FP4X4),
                 lhsT_scale=weight_scales[rows, i, M_TILE * m : M_TILE * (m + 1)],
                 rhs=x_codes[rows, window].bitcast(FP8X4),
                 rhs_scale=x_scales[rows, window],
@@ -116,14 +118,22 @@ def tile_rows_gglu_silu_kernel(tc, x, w_words, w_scales, u_words, u_scales, out)
         nc.vector.memset(weight_scales[:].rearrange("p i m -> p (i m)").bitcast(I32), 0)
         nc.vector.memset(x_codes[:, 0:PAD], 0)
         nc.vector.memset(x_scales[:, 0:PAD].bitcast(I32), 0)
-        load_words(W)
-        for g in range(G - 1):
-            load_scales(W, g)
+        first_tile, second_tile, both_tiles = slice(0, M_TILE), slice(M_TILE, M), slice(0, M)
+        last = G - 1
+        load_words(W, 0)
+        for g in range(last):
+            load_scales(W, g, first_tile)
         load_x(1)
-        load_scales(W, G - 1)
-        load_words(U)
-        for g in range(G):
-            load_scales(U, g)
+        load_words(U, 0)
+        load_scales(U, 0, both_tiles)
+        load_scales(W, last, first_tile)
+        for g in range(1, G):
+            load_scales(U, g, both_tiles)
+        load_words(W, 1)
+        load_scales(W, last, second_tile)
+        load_words(U, 1)
+        for g in range(last):
+            load_scales(W, g, second_tile)
 
         for h in range(len(CHUNKS)):
             prepare(h)
@@ -133,7 +143,7 @@ def tile_rows_gglu_silu_kernel(tc, x, w_words, w_scales, u_words, u_scales, out)
                 multiply(i, g)
 
         gates = [keep.tile([P, c1 - c0], F32, name=f"gate{k}") for k, (g, m, c0, c1) in enumerate(units)]
-        paired = (0, 2)
+        paired = ()
         results, pair_tiles = {}, {}
         for k, (g, m, c0, c1) in enumerate(units):
             if k - 1 in paired:
@@ -164,8 +174,12 @@ def tile_rows_gglu_silu_kernel(tc, x, w_words, w_scales, u_words, u_scales, out)
             if k + G < len(units):
                 multiply(U, k + G)
 
-        activate(0)
-        for k in range(1, len(units)):
+        for k in range(G):
+            activate(k)
+            if k >= 2:
+                combine(k - 2)
+        combine(G - 2)
+        for k in range(G, len(units)):
             activate(k)
             combine(k - 1)
         combine(len(units) - 1)

@@ -126,12 +126,13 @@ def tile_rows_gglu_silu_kernel(tc, x, w_words, w_scales, u_words, u_scales, out)
         load_x(1)
         load_words(U, 0)
         load_scales(U, 0, both_tiles)
-        load_scales(W, last, first_tile)
-        for g in range(1, G):
+        load_scales(W, last, both_tiles)
+        for g in range(1, last):
             load_scales(U, g, both_tiles)
+        load_scales(U, last, first_tile)
         load_words(W, 1)
-        load_scales(W, last, second_tile)
         load_words(U, 1)
+        load_scales(U, last, second_tile)
         for g in range(last):
             load_scales(W, g, second_tile)
 

@@ -24,7 +24,7 @@ CHUNKS = ((0, 128, 256), (256, 384, 512))
 FIRST = CHUNKS[0][-1]
 PAD = N - FIRST
 STEP = 256
-RUN = 4
+RUN = 2
 PAIR = 2
 W, U = 0, 1
 
@@ -144,22 +144,11 @@ def tile_rows_gglu_silu_kernel(tc, x, w_words, w_scales, u_words, u_scales, out)
                 multiply(i, g)
 
         gates = [keep.tile([P, c1 - c0], F32, name=f"gate{k}") for k, (g, m, c0, c1) in enumerate(units)]
-        paired = ()
-        results, pair_tiles = {}, {}
-        for k, (g, m, c0, c1) in enumerate(units):
-            if k - 1 in paired:
-                continue
-            count = 2 if k in paired else 1
-            tile = keep.tile([P, count, c1 - c0], F32, name=f"result{k}")
-            for place in range(count):
-                results.setdefault(k + place, tile[:, place, :])
-            pair_tiles.setdefault(k + count - 1, (k, tile))
+        results = [keep.tile([P, c1 - c0], F32, name=f"result{k}") for k, (g, m, c0, c1) in enumerate(units)]
 
         def store(k):
-            first, tile = pair_tiles[k]
-            g, m, c0, c1 = units[first]
-            rows = out[g : g + k - first + 1, M_TILE * m : M_TILE * (m + 1), c0:c1].rearrange("g m n -> m g n")
-            nc.sync.dma_start(out=rows, in_=tile[:])
+            g, m, c0, c1 = units[k]
+            nc.sync.dma_start(out=out[g, M_TILE * m : M_TILE * (m + 1), c0:c1], in_=results[k][:])
 
         def activate(k):
             for cols in steps(k):
@@ -170,8 +159,7 @@ def tile_rows_gglu_silu_kernel(tc, x, w_words, w_scales, u_words, u_scales, out)
         def combine(k):
             for cols in steps(k):
                 nc.vector.tensor_tensor(out=results[k][:, cols], in0=sums(U, k, cols), in1=gates[k][:, cols], op=MULT)
-            if k in pair_tiles:
-                store(k)
+            store(k)
             if k + G < len(units):
                 multiply(U, k + G)
 

@@ -26,6 +26,7 @@ PAD = N - FIRST
 STEP = 256
 RUN = 2
 PAIR = 2
+BURST = 256
 W, U = 0, 1
 
 
@@ -33,13 +34,10 @@ def tile_rows_gglu_silu_kernel(tc, x, w_words, w_scales, u_words, u_scales, out)
     nc = tc.nc
     with ExitStack() as ctx:
         keep = ctx.enter_context(tc.tile_pool(name="keep", bufs=1))
+        staged = ctx.enter_context(tc.tile_pool(name="staged", bufs=1))
         psum = ctx.enter_context(tc.psum_pool(name="psum", bufs=1))
         ctx.enter_context(tc.manual_schedule())
 
-        raw = [
-            [keep.tile([P, PAIR, c[-1] - c[0]], F32, name=f"raw{h}{j}", align_bytes=64) for j in range(PACK // PAIR)]
-            for h, c in enumerate(CHUNKS)
-        ]
         grouped = keep.tile([P, N, PACK], BF16, align_bytes=64)
         x_codes = keep.tile([P, PAD + N], U32, align_bytes=64)
         x_scales = keep.tile([P, PAD + N], U8, align_bytes=64)
@@ -48,6 +46,10 @@ def tile_rows_gglu_silu_kernel(tc, x, w_words, w_scales, u_words, u_scales, out)
             for i in (W, U)
         ]
         weight_scales = keep.tile([P, 2, M], U8, align_bytes=64)
+        raw = [
+            [staged.tile([P, PAIR, c[-1] - c[0]], F32, name=f"raw{h}{j}", align_bytes=BURST) for j in range(PACK // PAIR)]
+            for h, c in enumerate(CHUNKS)
+        ]
         banks = [[psum.tile([M_TILE, N], F32, name=f"bank{i}{g}") for g in range(G)] for i in (W, U)]
 
         x_rows = x.rearrange("g (p j) n -> (g p) j n", j=PACK)
@@ -144,7 +146,7 @@ def tile_rows_gglu_silu_kernel(tc, x, w_words, w_scales, u_words, u_scales, out)
                 multiply(i, g)
 
         gates = [keep.tile([P, c1 - c0], F32, name=f"gate{k}") for k, (g, m, c0, c1) in enumerate(units)]
-        results = [keep.tile([P, c1 - c0], F32, name=f"result{k}") for k, (g, m, c0, c1) in enumerate(units)]
+        results = [staged.tile([P, c1 - c0], F32, name=f"result{k}", align_bytes=BURST) for k, (g, m, c0, c1) in enumerate(units)]
 
         def store(k):
             g, m, c0, c1 = units[k]

@@ -22,7 +22,8 @@ SCALE_ROWS = D // 32
 M_TILE = 128
 CHUNKS = ((0, 128, 256), (256, 384, 512))
 FIRST = CHUNKS[0][-1]
-PAD = N - FIRST
+PAD = N
+WARM_UP = (2, 3)
 STEP = 256
 RUN = 2
 PAIR = 2
@@ -140,6 +141,18 @@ def tile_rows_gglu_silu_kernel(tc, x, w_words, w_scales, u_words, u_scales, out)
 
         for h in range(len(CHUNKS)):
             prepare(h)
+
+        for g in WARM_UP:
+            rows = slice(ROWS * g, ROWS * (g + 1))
+            nc.tensor.matmul_mx(
+                out=banks[U][g][:],
+                lhsT=words[W][0][rows, :].bitcast(FP4X4),
+                lhsT_scale=x_scales[rows, 0:M_TILE],
+                rhs=x_codes[rows, 0:N].bitcast(FP8X4),
+                rhs_scale=x_scales[rows, 0:N],
+                start=True,
+                stop=True,
+            )
 
         for i in (W, U):
             for g in range(G):

@@ -63,10 +63,9 @@ def tile_rows_gglu_silu_kernel(tc, x, w_words, w_scales, u_words, u_scales, out)
             src = (w_words, u_words)[i].rearrange("g p b -> (g p) b")[:, 2 * M_TILE * m : 2 * M_TILE * (m + 1)]
             nc.sync.dma_start(out=words[i][m][:].bitcast(I32), in_=src.bitcast(I32))
 
-        def load_scales(i, g, outputs):
-            src = (w_scales, u_scales)[i][g][:, outputs]
+        def load_scales(i, g):
             rows = slice(ROWS * g, ROWS * g + SCALE_ROWS)
-            nc.sync.dma_start(out=weight_scales[rows, i, outputs].bitcast(I32), in_=src.bitcast(I32))
+            nc.sync.dma_start(out=weight_scales[rows, i, :].bitcast(I32), in_=(w_scales, u_scales)[i][g].bitcast(I32))
 
         def interleave(h, j, c0, c1):
             nc.vector.tensor_copy(
@@ -121,23 +120,18 @@ def tile_rows_gglu_silu_kernel(tc, x, w_words, w_scales, u_words, u_scales, out)
         nc.vector.memset(weight_scales[:].rearrange("p i m -> p (i m)").bitcast(I32), 0)
         nc.vector.memset(x_codes[:, 0:PAD], 0)
         nc.vector.memset(x_scales[:, 0:PAD].bitcast(I32), 0)
-        first_tile, second_tile, both_tiles = slice(0, M_TILE), slice(M_TILE, M), slice(0, M)
         last = G - 1
         load_words(W, 0)
         for g in range(last):
-            load_scales(W, g, first_tile)
+            load_scales(W, g)
         load_x(1)
         load_words(U, 0)
-        load_scales(U, 0, both_tiles)
-        load_scales(W, last, both_tiles)
-        for g in range(1, last):
-            load_scales(U, g, both_tiles)
-        load_scales(U, last, first_tile)
+        load_scales(U, 0)
+        load_scales(W, last)
+        for g in range(1, G):
+            load_scales(U, g)
         load_words(W, 1)
         load_words(U, 1)
-        load_scales(U, last, second_tile)
-        for g in range(last):
-            load_scales(W, g, second_tile)
 
         for h in range(len(CHUNKS)):
             prepare(h)
@@ -161,9 +155,9 @@ def tile_rows_gglu_silu_kernel(tc, x, w_words, w_scales, u_words, u_scales, out)
         gates = [keep.tile([P, c1 - c0], F32, name=f"gate{k}") for k, (g, m, c0, c1) in enumerate(units)]
         results = [staged.tile([P, c1 - c0], F32, name=f"result{k}", align_bytes=BURST) for k, (g, m, c0, c1) in enumerate(units)]
 
-        def store(k):
+        def store(k, cols):
             g, m, c0, c1 = units[k]
-            nc.sync.dma_start(out=out[g, M_TILE * m : M_TILE * (m + 1), c0:c1], in_=results[k][:])
+            nc.sync.dma_start(out=out[g, M_TILE * m : M_TILE * (m + 1), c0:c1][:, cols], in_=results[k][:, cols])
 
         def activate(k):
             for cols in steps(k):
@@ -174,7 +168,7 @@ def tile_rows_gglu_silu_kernel(tc, x, w_words, w_scales, u_words, u_scales, out)
         def combine(k):
             for cols in steps(k):
                 nc.vector.tensor_tensor(out=results[k][:, cols], in0=sums(U, k, cols), in1=gates[k][:, cols], op=MULT)
-            store(k)
+                store(k, cols)
             if k + G < len(units):
                 multiply(U, k + G)
 

@@ -25,6 +25,7 @@ FIRST = CHUNKS[0][-1]
 PAD = N
 WARM_UP = (2, 3)
 STEP = 256
+LAST_STEP = 128
 RUN = 2
 PAIR = 2
 BURST = 256
@@ -109,7 +110,7 @@ def tile_rows_gglu_silu_kernel(tc, x, w_words, w_scales, u_words, u_scales, out)
 
         def steps(k):
             width = units[k][3] - units[k][2]
-            count = -(-width // STEP)
+            count = -(-width // (STEP if k + 1 < len(units) else LAST_STEP))
             return [slice(s * width // count, (s + 1) * width // count) for s in range(count)]
 
         def sums(i, k, cols):
@@ -168,7 +169,10 @@ def tile_rows_gglu_silu_kernel(tc, x, w_words, w_scales, u_words, u_scales, out)
         def combine(k):
             for cols in steps(k):
                 nc.vector.tensor_tensor(out=results[k][:, cols], in0=sums(U, k, cols), in1=gates[k][:, cols], op=MULT)
-                store(k, cols)
+                if k + 1 < len(units):
+                    store(k, cols)
+            if k + 1 == len(units):
+                store(k, slice(None))
             if k + G < len(units):
                 multiply(U, k + G)
 

@@ -42,12 +42,13 @@ def tile_rows_gglu_silu_kernel(tc, x, w_words, w_scales, u_words, u_scales, out)
 
         grouped = keep.tile([P, N, PACK], BF16, align_bytes=64)
         x_codes = keep.tile([P, PAD + N], U32, align_bytes=64)
-        x_scales = keep.tile([P, PAD + N], U8, align_bytes=64)
+        scales = keep.tile([P, 2 * M + PAD + N], U8, align_bytes=64)
+        weight_scales = [scales[:, M * i : M * (i + 1)] for i in (W, U)]
+        x_scales = scales[:, 2 * M :]
         words = [
             [keep.tile([P, 2 * M_TILE], U8, name=f"words{i}{m}", align_bytes=64) for m in range(M // M_TILE)]
             for i in (W, U)
         ]
-        weight_scales = keep.tile([P, 2, M], U8, align_bytes=64)
         raw = [
             [staged.tile([P, PAIR, c[-1] - c[0]], F32, name=f"raw{h}{j}", align_bytes=BURST) for j in range(PACK // PAIR)]
             for h, c in enumerate(CHUNKS)
@@ -66,7 +67,7 @@ def tile_rows_gglu_silu_kernel(tc, x, w_words, w_scales, u_words, u_scales, out)
 
         def load_scales(i, g):
             rows = slice(ROWS * g, ROWS * g + SCALE_ROWS)
-            nc.sync.dma_start(out=weight_scales[rows, i, :].bitcast(I32), in_=(w_scales, u_scales)[i][g].bitcast(I32))
+            nc.sync.dma_start(out=weight_scales[i][rows, :].bitcast(I32), in_=(w_scales, u_scales)[i][g].bitcast(I32))
 
         def interleave(h, j, c0, c1):
             nc.vector.tensor_copy(
@@ -101,7 +102,7 @@ def tile_rows_gglu_silu_kernel(tc, x, w_words, w_scales, u_words, u_scales, out)
             nc.tensor.matmul_mx(
                 out=banks[i][g][:],
                 lhsT=words[i][m][rows, :].bitcast(FP4X4),
-                lhsT_scale=weight_scales[rows, i, M_TILE * m : M_TILE * (m + 1)],
+                lhsT_scale=weight_scales[i][rows, M_TILE * m : M_TILE * (m + 1)],
                 rhs=x_codes[rows, window].bitcast(FP8X4),
                 rhs_scale=x_scales[rows, window],
                 start=True,
@@ -118,9 +119,8 @@ def tile_rows_gglu_silu_kernel(tc, x, w_words, w_scales, u_words, u_scales, out)
             return banks[i][g][:, N - (c1 - c0) : N][:, cols]
 
         load_x(0)
-        nc.vector.memset(weight_scales[:].rearrange("p i m -> p (i m)").bitcast(I32), 0)
+        nc.vector.memset(scales[:, 0 : 2 * M + PAD].bitcast(I32), 0)
         nc.vector.memset(x_codes[:, 0:PAD], 0)
-        nc.vector.memset(x_scales[:, 0:PAD].bitcast(I32), 0)
         last = G - 1
         load_words(W, 0)
         for g in range(last):

from contextlib import ExitStack

import concourse.mybir as mybir

G, D, M, N = 4, 128, 256, 512
FLOPS = 2 * 2 * G * D * M * N

F32 = mybir.dt.float32
BF16 = mybir.dt.bfloat16
I32 = mybir.dt.int32
U32 = mybir.dt.uint32
U8 = mybir.dt.uint8
FP8X4 = mybir.dt.float8_e4m3fn_x4
FP4X4 = mybir.dt.float4_e2m1fn_x4
SILU = mybir.ActivationFunctionType.Silu
MULT = mybir.AluOpType.mult

P = 128
PACK = 4
ROWS = D // PACK
SCALE_ROWS = D // 32
M_TILE = 128
CHUNKS = ((0, 128, 256), (256, 384, 512))
FIRST = CHUNKS[0][-1]
PAD = N
WARM_UP = (2, 3)
STEP = 256
LAST_STEP = 128
RUN = 2
PAIR = 2
BURST = 256
W, U = 0, 1


def tile_rows_gglu_silu_kernel(tc, x, w_words, w_scales, u_words, u_scales, out):
    nc = tc.nc
    with ExitStack() as ctx:
        keep = ctx.enter_context(tc.tile_pool(name="keep", bufs=1))
        staged = ctx.enter_context(tc.tile_pool(name="staged", bufs=1))
        psum = ctx.enter_context(tc.psum_pool(name="psum", bufs=1))
        ctx.enter_context(tc.manual_schedule())

        grouped = keep.tile([P, N, PACK], BF16, align_bytes=64)
        x_codes = keep.tile([P, PAD + N], U32, align_bytes=64)
        scales = keep.tile([P, 2 * M + PAD + N], U8, align_bytes=64)
        weight_scales = [scales[:, M * i : M * (i + 1)] for i in (W, U)]
        x_scales = scales[:, 2 * M :]
        words = [
            [keep.tile([P, 2 * M_TILE], U8, name=f"words{i}{m}", align_bytes=64) for m in range(M // M_TILE)]
            for i in (W, U)
        ]
        raw = [
            [staged.tile([P, PAIR, c[-1] - c[0]], F32, name=f"raw{h}{j}", align_bytes=BURST) for j in range(PACK // PAIR)]
            for h, c in enumerate(CHUNKS)
        ]
        banks = [[psum.tile([M_TILE, N], F32, name=f"bank{i}{g}") for g in range(G)] for i in (W, U)]

        x_rows = x.rearrange("g (p j) n -> (g p) j n", j=PACK)

        def load_x(h):
            for j, tile in enumerate(raw[h]):
                nc.sync.dma_start(out=tile[:], in_=x_rows[:, PAIR * j : PAIR * (j + 1), CHUNKS[h][0] : CHUNKS[h][-1]])

        def load_words(i, m):
            src = (w_words, u_words)[i].rearrange("g p b -> (g p) b")[:, 2 * M_TILE * m : 2 * M_TILE * (m + 1)]
            nc.sync.dma_start(out=words[i][m][:].bitcast(I32), in_=src.bitcast(I32))

        def load_scales(i, g):
            rows = slice(ROWS * g, ROWS * g + SCALE_ROWS)
            nc.sync.dma_start(out=weight_scales[i][rows, :].bitcast(I32), in_=(w_scales, u_scales)[i][g].bitcast(I32))

        def interleave(h, j, c0, c1):
            nc.vector.tensor_copy(
                out=grouped[:, c0:c1, PAIR * j : PAIR * (j + 1)].rearrange("p (c i) j -> p c j i", i=RUN),
                in_=raw[h][j][:, :, c0 - CHUNKS[h][0] : c1 - CHUNKS[h][0]].rearrange("p j (c i) -> p c j i", i=RUN),
            )

        def quantize(c0, c1):
            nc.vector.quantize_mx(
                out=x_codes[:, PAD + c0 : PAD + c1].bitcast(FP8X4),
                scales=x_scales[:, PAD + c0 : PAD + c1],
                in_=grouped[:, c0:c1, :].rearrange("p n j -> p (n j)"),
            )

        def prepare(h):
            pieces = list(zip(CHUNKS[h], CHUNKS[h][1:]))
            interleave(h, 0, CHUNKS[h][0], CHUNKS[h][-1])
            for c0, c1 in pieces:
                interleave(h, 1, c0, c1)
            for c0, c1 in pieces:
                quantize(c0, c1)

        early = [(g, 0, 0, FIRST) for g in range(G)]
        late = [(g, 0, FIRST, N) for g in range(G)]
        whole = [(g, 1, 0, N) for g in range(G)]
        units = early + late[:-1] + whole[-1:] + whole[:-1] + late[-1:]

        def multiply(i, k):
            g, m, c0, c1 = units[k]
            rows = slice(ROWS * g, ROWS * (g + 1))
            window = slice(PAD + c1 - N, PAD + c1)
            nc.tensor.matmul_mx(
                out=banks[i][g][:],
                lhsT=words[i][m][rows, :].bitcast(FP4X4),
                lhsT_scale=weight_scales[i][rows, M_TILE * m : M_TILE * (m + 1)],
                rhs=x_codes[rows, window].bitcast(FP8X4),
                rhs_scale=x_scales[rows, window],
                start=True,
                stop=True,
            )

        def steps(k):
            width = units[k][3] - units[k][2]
            count = -(-width // (STEP if k + 1 < len(units) else LAST_STEP))
            return [slice(s * width // count, (s + 1) * width // count) for s in range(count)]

        def sums(i, k, cols):
            g, m, c0, c1 = units[k]
            return banks[i][g][:, N - (c1 - c0) : N][:, cols]

        load_x(0)
        nc.vector.memset(scales[:, 0 : 2 * M + PAD].bitcast(I32), 0)
        nc.vector.memset(x_codes[:, 0:PAD], 0)
        last = G - 1
        load_words(W, 0)
        for g in range(last):
            load_scales(W, g)
        load_x(1)
        load_words(U, 0)
        load_scales(U, 0)
        load_scales(W, last)
        for g in range(1, G):
            load_scales(U, g)
        load_words(W, 1)
        load_words(U, 1)

        for h in range(len(CHUNKS)):
            prepare(h)

        for g in WARM_UP:
            rows = slice(ROWS * g, ROWS * (g + 1))
            nc.tensor.matmul_mx(
                out=banks[U][g][:],
                lhsT=words[W][0][rows, :].bitcast(FP4X4),
                lhsT_scale=x_scales[rows, 0:M_TILE],
                rhs=x_codes[rows, 0:N].bitcast(FP8X4),
                rhs_scale=x_scales[rows, 0:N],
                start=True,
                stop=True,
            )

        for i in (W, U):
            for g in range(G):
                multiply(i, g)

        gates = [keep.tile([P, c1 - c0], F32, name=f"gate{k}") for k, (g, m, c0, c1) in enumerate(units)]
        results = [staged.tile([P, c1 - c0], F32, name=f"result{k}", align_bytes=BURST) for k, (g, m, c0, c1) in enumerate(units)]

        def store(k, cols):
            g, m, c0, c1 = units[k]
            nc.sync.dma_start(out=out[g, M_TILE * m : M_TILE * (m + 1), c0:c1][:, cols], in_=results[k][:, cols])

        def activate(k):
            for cols in steps(k):
                nc.scalar.activation(out=gates[k][:, cols], in_=sums(W, k, cols), func=SILU)
            if k + G < len(units):
                multiply(W, k + G)

        def combine(k):
            for cols in steps(k):
                nc.vector.tensor_tensor(out=results[k][:, cols], in0=sums(U, k, cols), in1=gates[k][:, cols], op=MULT)
                if k + 1 < len(units):
                    store(k, cols)
            if k + 1 == len(units):
                store(k, slice(None))
            if k + G < len(units):
                multiply(U, k + G)

        for k in range(G):
            activate(k)
            if k >= 2:
                combine(k - 2)
        combine(G - 2)
        for k in range(G, len(units)):
            activate(k)
            combine(k - 1)
        combine(len(units) - 1)
